import numpy as np, ml_dtypes
CORES = [23,119,17,113]
N = 4
BF = ml_dtypes.bfloat16
def gentries(a):
    return np.ascontiguousarray(a.reshape(8, 16, -1).transpose(0, 2, 1)).reshape(8, -1)
def gtable(e):
    e = np.asarray(e); return np.ascontiguousarray(e.reshape(8, -1, 16).transpose(0, 2, 1)).reshape(128, -1).astype(np.int32)
T, C, E, D = 4096, 1024, 64, 6
def ints(rng, *shape):
    return rng.integers(-15, 16, shape).astype(np.float32).astype(BF)
def uneven(rng, *shape):
    s = rng.choice(np.array([0, 1, 3, 7, 15, 15]), shape[:-2] + (1, shape[-1]))
    return ((rng.integers(-15, 16, shape) * s) // 15).astype(np.float32).astype(BF)
def trees(rng, out, alone, tight, across):
    H = T // 2; i = np.arange(T); r = np.arange(N)[:, None, None]
    back = np.where(rng.random((N, 8, T)) < 0.5, rng.integers(1, 9, (N, 8, T)), 1 + np.floor(i * rng.random((N, 8, T))).astype(np.int64))
    pa = np.maximum(i - back, 0)
    pa = np.where(rng.random((N, 8, T)) < alone, i, pa)
    pa = np.where((rng.random((N, 8, T)) < out) & (i >= H) & (r > 0), T + rng.integers(0, E, (N, 8, T)), pa)
    at = rng.integers(0, H, (N, 8, E))
    if tight:
        w = H + np.arange(tight * D).reshape(tight, D)
        pa[:, :, w[:, :-1].reshape(-1)] = w[:, 1:].reshape(-1)
        pa[:, :, w[:, -1]] = np.where(r > 0, T + rng.integers(0, E, (N, 8, tight)), rng.integers(0, H, (N, 8, tight)))
        at[:, :, :tight] = w[:, 0]
    at = rng.permuted(at, axis=2)
    num = rng.permuted(np.tile(i, (N, 8, 1)), axis=2)
    par = np.zeros((N, 8, T), np.int64)
    np.put_along_axis(par, num, np.where(pa < T, np.take_along_axis(num, np.minimum(pa, T - 1), 2), pa), 2)
    ex = np.take_along_axis(np.roll(num, 1, axis=0), at, 2)
    u = np.where(rng.random((N, 8, C)) < 0.75, rng.integers(H, T, (N, 8, C)), rng.integers(0, T, (N, 8, C)))
    up = np.take_along_axis(num, u, 2)
    up = np.where((rng.random((N, 8, C)) < across) & (r > 0), T + rng.integers(0, E, (N, 8, C)), up)
    return up, par, ex
def pack(rng, up, par, ex):
    ex = ex.copy(); ex[0] = rng.integers(0, T, (8, E))
    return {"q": ints(rng, N, 128, C), "k": ints(rng, N, 128, T), "v": ints(rng, N, 128, T), "b": rng.integers(-15, 16, (N, 128, D)).astype(np.float32),
            "up": np.stack([gtable(a) for a in up]), "par": par.astype(np.int32), "ex": np.stack([gtable(a) for a in ex])}
def setup_inputs(rng):
    return pack(rng, *trees(rng, 0.125, 0.015625, E // 4, 0.125))
def setup_inputs_roots(rng):
    up, par, ex = trees(rng, 0.125, 0.5, 0, 0.125)
    par[:, :, 0] = 0; par[:, :, T - 1] = T - 1; par[:, :, 1] = 2; par[:, :, 2] = 3; par[:, :, 3] = 1
    ex[:, :, 0] = 0; ex[:, :, E - 1] = T - 1; ex[:, :, 1] = 1
    up[:, :, 0] = 0; up[:, :, 1] = T - 1; up[:, :, 2] = 1
    up[1:, :, 3] = T; up[1:, :, 4] = T + 1; up[1:, :, C - 1] = T + E - 1; up[0, :, C - 1] = T - 1
    return pack(rng, up, par, ex)
def setup_inputs_brink(rng):
    return pack(rng, *trees(rng, 0.5, 0.015625, E, 0.5))
def setup_inputs_alike(rng):
    up, par, ex = trees(rng, 0.25, 0.015625, 0, 0.0)
    up = np.repeat(up[:, :, :1], C, axis=2); ex = np.repeat(ex[:, :, :1], E, axis=2)
    up[rng.integers(1, N)] = T + rng.integers(0, E, (8, 1))
    return pack(rng, up, par, ex)
def setup_inputs_spread(rng):
    d = setup_inputs(rng)
    d["q"] = uneven(rng, N, 128, C); d["k"] = uneven(rng, N, 128, T); d["v"] = uneven(rng, N, 128, T)
    d["b"] = rng.choice(np.array([-15, -1, 0, 0, 1, 15]), (N, 128, D)).astype(np.float32); return d
def check_inputs(d):
    bad = []
    for n in ("q", "k", "v", "b"):
        w = d[n].astype(np.float32)
        if not ((np.abs(w) <= 15) & (w == np.rint(w))).all(): bad.append(n + ": whole numbers from -15 to 15")
    for n in ("up", "par"):
        w = d[n]
        if w.min() < 0 or w.max() >= T + E or w[0].max() >= T: bad.append(n + ": range")
    if d["ex"].min() < 0 or d["ex"].max() >= T: bad.append("ex: range")
    if bad: return bad
    for r in range(1, N):
        a = gentries(d["ex"][r]).astype(np.int64)
        for t in range(D - 1):
            a = np.take_along_axis(d["par"][r - 1], a, 1).astype(np.int64)
            if (a >= T).any(): return ["the nodes above an exit's node"]
    return bad
def reference(q, k, v, b, up, par, ex):
    y = np.zeros((N, 128, C), np.float32)
    u = np.stack([gentries(a) for a in up]).astype(np.int64); x = np.stack([gentries(a) for a in ex]).astype(np.int64)
    def place(m, r, g):
        return np.where(m < T, r * T + m, (r - 1) * T + x[r, g][np.maximum(m - T, 0)])
    for g in range(8):
        s = slice(16 * g, 16 * g + 16)
        above = np.concatenate([place(par[r, g].astype(np.int64), r, g) for r in range(N)])
        kk = np.concatenate([k[r, s].astype(np.float32) for r in range(N)], axis=1); vv = np.concatenate([v[r, s].astype(np.float32) for r in range(N)], axis=1)
        for r in range(N):
            a = place(u[r, g], r, g); qq = q[r, s].astype(np.float32)
            for t in range(D):
                y[r, s] += np.maximum(qq - kk[:, a] + b[r, s, t:t + 1], np.float32(0)) * vv[:, a]
                a = above[a]
    return {"y": y}

@@ -1,0 +1,332 @@
+from concourse.mybir import AluOpType, ActivationFunctionType
+
+NT, NQ, NE, ND = 4096, 1024, 64, 6
+WIN = NT + NE * ND
+PW = NT + NE * (ND - 1)
+K1, V1 = 3072, 3072
+ZS = 1024
+
+SCRATCH = {
+    "kwin": ("sbuf", [128, WIN], "bfloat16"), "vwin": ("sbuf", [128, WIN], "bfloat16"),
+    "pwin": ("sbuf", [128, PW], "bfloat16"),
+    "parc": ("sbuf", [128, 256], "int32"), "hi": ("sbuf", [128, 256], "bfloat16"), "lo": ("sbuf", [128, 256], "bfloat16"),
+    "upc": ("sbuf", [128, 64], "int32"), "exs": ("sbuf", [128, 4], "int32"), "exl": ("sbuf", [128, 4], "int32"),
+    "off": ("sbuf", [128, 8, 72], "uint16"), "xla": ("sbuf", [128, 24], "uint16"), "xlb": ("sbuf", [128, 24], "uint16"),
+    "res": ("sbuf", [128, 6, 1088], "bfloat16"),
+    "cst": ("sbuf", [128, 400], "bfloat16"), "elo": ("sbuf", [128, 320], "bfloat16"),
+    "qs": ("sbuf", [128, NQ], "bfloat16"), "bs": ("sbuf", [128, 8], "float32"), "bb": ("sbuf", [128, 8], "bfloat16"),
+    "tk": ("sbuf", [128, 6, NQ], "bfloat16"), "rl": ("sbuf", [128, 6, NQ], "bfloat16"), "vg": ("sbuf", [128, 6, NQ], "bfloat16"),
+    "pr": ("sbuf", [128, 6, NQ], "float16"), "yo": ("sbuf", [128, NQ], "float32"),
+    "xk": ("sbuf", [128, NE * ND], "bfloat16"), "xv": ("sbuf", [128, NE * ND], "bfloat16"),
+    "accA": ("psum", [128, 512], "float32"), "accB1": ("psum", [128, 512], "float32"), "accB2": ("psum", [128, 512], "float32"),
+    "chA": ("psum", [128, 512], "float32"), "chB": ("psum", [128, 512], "float32"),
+    "a0": ("psum", [128, 512], "float32"), "a1": ("psum", [128, 512], "float32"), "a2": ("psum", [128, 512], "float32"),
+}
+
+TYPES = "VTVTSZVSSSWZ"
+MODE = "HHHHA"
+GK = [1, 1, 1, 0, 1, 0]
+GV = [1, 0, 0, 1, 0, 0]
+XE = "SSSSSVSVVSSVS"
+KMSG = [[0], [1], [2], [3, 4, 5]]
+VMSG = [[0, 1, 2], [3, 4, 5]]
+ORDER = ("C1Bs C1As C1Bv P1B C1Av cpX cp1B P1A C2Bs C2Bv xk0 cp1A C2Av C2As P2B cp2B P2A C3Bv mk0 C3Bs cp2A xk1 P3B C3Av "
+         "mk1 cp3B C3As C4Bs C4Bv P3A cp3A P4B xk2 C4As xl02 C4Av P4A mk2 cp4B K1F C5Bs cp4A xv0 P5B R1F mv0 cp5B K2F C6Bv "
+         "P6B cp6B K3B xl35 R2F K3A xk3 a3B C5As R3B V1F G3B V2A V2B a3A V3B P5A xv3 cp5A mk3 K4A R3A K5A s1F s2A s2B s3B "
+         "a5A K4B a4B K6A mv3 R4A K5B K6B R5A R6A V3A V4A R4B V5A a5B a6B R6B V6A V4B s3A R5B s5A G6B s4A s6A V5B V6B2 s4B "
+         "s5B V6B1 fA fB2 yA yB2 s6B1 fB1 yB1").split()
+
+ARR = ["a_ex"] + ["a_k%d" % m[0] for m in KMSG] + ["a_v%d" % m[0] for m in VMSG]
+SEMAPHORES = ["sent"] + ARR + ["s%d" % i for i in range(149 - len(ARR))]
+
+
+def rank_program(g, core, T, topo):
+    rank = T.rank_of(core)
+    if rank is None:
+        return
+    N = len(T.cores)
+    takes = rank > 0
+    gives = rank < N - 1
+    A, F = AluOpType, ActivationFunctionType
+    Q = {"V": g.vector, "S": g.scalar, "P": g.tensor, "G": g, "Y": g.sync}
+    ops = {}
+
+    def add(name, q, fn, deps, inc=1):
+        ops[name] = (q, fn, list(deps), inc)
+
+    def dma(name, q, out, in_, deps):
+        add(name, q, lambda: Q[q].dma_start(out, in_), deps, 16)
+
+    sent = [0]
+
+    def send(name, dst, out, in_, sem, deps):
+        rid, pid = topo.addr(dst)[0:2]
+        sent[0] += len(topo.engines(core, dst))
+        add(name, "G", lambda: g.remote_dma(out, in_, T.sem[sem], T.sem.sent, pid, rid, topo.mask(core, dst)), deps, 0)
+
+    arrive = {}
+    if gives:
+        arrive["a_ex"] = len(topo.engines(T.cores[rank + 1], core))
+    if takes:
+        for a in ARR[1:]:
+            arrive[a] = len(topo.engines(T.cores[rank - 1], core))
+
+    def gather(e, out, win, offs):
+        if e == "V":
+            return lambda: g.vector.tensor_copy(out, win.indirect(offs))
+        return lambda: g.scalar.activation(out, win.indirect(offs), F.Copy)
+
+    Wm, Id, nId = T.cst[:, 0:144], T.cst[:, 144:272], T.cst[:, 272:400]
+
+    if takes:
+        dma("dex", "S", T.exs[:], T.ex[:], [])
+    dma("dpar", "Y", T.parc[:], T.par[:], [])
+    dma("dup", "S", T.upc[:], T.up[:], [])
+    dma("dk1", "Y", T.kwin[:, 0:K1], T.k[:, 0:K1], [])
+    dma("db", "S", T.bs[:, 0:ND], T.b[:], [])
+    add("ms0", "V", lambda: g.vector.memset(T.pwin[:, 0:ZS], 0.0), [])
+    add("ms", "V", lambda: g.vector.memset(T.pwin[:, ZS:NT - ZS], 0.0), [])
+    add("mss", "S", lambda: g.scalar.activation(T.pwin[:, NT - ZS:NT], T.pwin[:, 0:ZS], F.Copy), ["ms0"])
+    win = ["dhi", "dlo"]
+    if takes:
+        add("io1", "G", lambda: g.iota(T.pwin[:, NT:PW], [[NE, ND - 1], [0, NE]], NT + NE, 0, allow_small_or_imprecise_dtypes=True), [])
+        add("io2", "G", lambda: g.iota(T.elo[:], [[0, ND - 1], [1, NE]], 0, 0, allow_small_or_imprecise_dtypes=True), [])
+        dma("delo", "S", T.pwin[1:128:16, NT:PW], T.elo[0:8, :], ["io1", "io2"])
+        send("mex", T.cores[rank - 1], T.exl[:], T.exs[:], "a_ex", ["dex"])
+        win.append("delo")
+    add("hi", "V", lambda: g.vector.tensor_copy(T.hi[:], T.parc[:]), ["dpar"])
+    dma("dhi", "Y", T.pwin[0:128:16, 0:NT], T.hi[:], ["hi", "ms", "mss"])
+    add("lo", "V", lambda: g.vector.tensor_tensor(T.lo[:], T.parc[:], T.hi[:], A.subtract), ["hi"])
+    dma("dlo", "S", T.pwin[1:128:16, 0:NT], T.lo[:], ["lo", "ms", "mss"])
+    dma("dk2", "Y", T.kwin[:, K1:NT], T.k[:, K1:NT], [])
+    dma("dq", "Y", T.qs[:], T.q[:], [])
+    add("msc", "V", lambda: g.vector.memset(T.cst[:], 0.0), [])
+    add("cpU", "V", lambda: g.vector.tensor_copy(T.off[:, 1, 0:64], T.upc[:]), ["dup"])
+    add("bb", "V", lambda: g.vector.tensor_copy(T.bb[:, 0:ND], T.bs[:, 0:ND]), ["db"])
+    add("W1", "G", lambda: g.affine_select(Wm, Wm, [[-16, 9], [-1000, 16]], A.not_equal, 1.0, 16, 1), ["msc"])
+    add("W2", "G", lambda: g.affine_select(Wm, Wm, [[-16, 9], [-1000, 16]], A.not_equal, 1.0, 15, 1), ["W1"])
+    add("Id", "G", lambda: g.affine_select(Id, Id, [[-1, 128]], A.not_equal, 1.0, 0, 1), ["msc"])
+    add("nId", "G", lambda: g.affine_select(nId, nId, [[-1, 128]], A.not_equal, -1.0, 0, 1), ["msc"])
+    if gives:
+        dma("dv1", "Y", T.vwin[:, 0:V1], T.v[:, 0:V1], ["dhi", "dlo"])
+        pre = list(ops)
+        dma("dv2", "Y", T.vwin[:, V1:NT], T.v[:, V1:NT], ["xk0"])
+        ld = {"k": ["dk1", "dk2"], "v": ["dv1", "dv2"]}
+    else:
+        dma("dv1", "Y", T.vwin[:, 0:NT], T.v[:], ["dhi", "dlo"])
+        pre = list(ops)
+        ld = {"k": ["dk1", "dk2"], "v": ["dv1"]}
+
+    def ready(s, h):
+        if s == 1:
+            return ["cpU"]
+        if s == 7:
+            return ["cp6B"]
+        if MODE[s - 2] in "FSV":
+            return ["cp%dF" % (s - 1)]
+        return ["cp%d%s" % (s - 1, x) for x in ("AB" if h == "F" else h)]
+
+    def xready(t):
+        return ["cpX"] if t == 0 else ready(t + 2, "B")
+
+    pwin = T.pwin[:, 0:(PW if takes else NT)]
+
+    def relay(name, s, c0, c1, r0, ps, deps):
+        n = c1 - c0
+
+        def emit():
+            for i in range(16):
+                ins = g.tensor.matmul(ps[:, 0:n], T.cst[:, 16 - i:144 - i], T.res[:, s - 1, r0 + i:r0 + 16 * n:16], i == 0, i == 15)
+            return ins
+        add("P" + name, "P", emit, deps + ["W2"])
+        add("cp" + name, "V", lambda: g.vector.tensor_copy(T.off[:, s + 1, c0:c1], ps[:, 0:n]), ["P" + name])
+
+    if gives:
+        add("cpX", "V", lambda: g.vector.tensor_copy(T.off[:, 2, 64:68], T.exl[:]), ["a_ex"])
+    for s in range(1, ND):
+        m = MODE[s - 1]
+        end = 68 if (s > 1 and gives) else 64
+        for h in ("F" if m in "FSV" else "AB"):
+            c0, c1 = {"F": (0, end), "A": (0, 32), "B": (32, end)}[h]
+            d = ready(s, h) + win + (["cpX"] if s == 2 and h != "A" and gives else [])
+            es = {"H": "vs", "F": "vs", "S": "s", "A": "s", "V": "v", "B": "v" if h == "A" else "s"}[m]
+            cuts = [c0, c1] if len(es) == 1 else [c0, (c0 + c1) // 2, c1]
+            for j, e in enumerate(es):
+                a, b = cuts[j], cuts[j + 1]
+                add("C%d%s%s" % (s, h, e), e.upper(), gather(e.upper(), T.res[:, s - 1, 16 * a:16 * b], pwin, T.off[:, s, a:b]), d)
+            relay("%d%s" % (s, h), s, c0, c1, 16 * c0, T.chB if h == "B" else T.chA, ["C%d%s%s" % (s, h, e) for e in es])
+    if gives:
+        add("C6Bv", XE[12], gather(XE[12], T.res[:, 5, 0:64], pwin, T.off[:, 6, 64:68]), ready(6, "B"))
+        relay("6B", 6, 64, 68, 0, T.chB, ["C6Bv"])
+
+    arr = {"k": {}, "v": {}}
+    lists = {}
+    for nm, msgs, wn, st in (("k", KMSG, T.kwin, T.xk), ("v", VMSG, T.vwin, T.xv)):
+        for m in msgs:
+            a, b = m[0], m[-1] + 1
+            for t in m:
+                arr[nm][t] = "a_%s%d" % (nm, a)
+            if not gives:
+                continue
+            if len(m) > 1:
+                key = "xl%d%d" % (a, b - 1)
+                if key not in lists:
+                    xl = (T.xla if nm == "k" else T.xlb)[:, 4 * a:4 * b]
+                    lists[key] = xl
+                    add(key, "V", (lambda o, i: lambda: g.vector.tensor_copy(o, i))(xl, T.off[:, a + 2:b + 2, 64:68]),
+                        sum([xready(t) for t in m], []))
+                d, offs = [key], lists[key]
+            else:
+                d, offs = xready(a), T.off[:, a + 2, 64:68]
+            e = XE[a + (6 if nm == "v" else 0)]
+            add("x%s%d" % (nm, a), e, gather(e, st[:, NE * a:NE * b], wn[:, 0:NT], offs), d + ld[nm])
+            send("m%s%d" % (nm, a), T.cores[rank + 1], wn[:, NT + NE * a:NT + NE * b], st[:, NE * a:NE * b],
+                 "a_%s%d" % (nm, a), ["x%s%d" % (nm, a)])
+
+    apos = [n for n in ORDER if n[0] == "a"]
+    banks = [T.a0, T.a1, T.a2]
+    cols = {"F": (0, 1024), "A": (0, 512), "B": (512, 1024), "B1": (512, 768), "B2": (768, 1024)}
+    acc = {"A": T.accA[:, 0:512], "B1": T.accB1[:, 0:256], "B2": T.accB2[:, 0:256]}
+    sums = {}
+
+    def level(s):
+        fk = GK[s - 1] and TYPES[2 * s - 2] in "VW"
+        ty = {h: TYPES[2 * s - 2 + (1 if h == "B" and not fk else 0)] for h in "ABF"}
+        wcols = NT + NE * s if takes else NT
+        kw, vw = T.kwin[:, 0:wcols], T.vwin[:, 0:wcols]
+        came = {x: (sorted(set(arr[x][i] for i in range(s))) if takes else []) for x in "kv"}
+        bcol, bbcol = T.bs[:, s - 1:s], T.bb[:, s - 1:s]
+        held = {}
+
+        def keys(h):
+            n = "%d%s" % (s, h)
+            c0, c1 = cols[h]
+            offs, tk, rl, qq = T.off[:, s, c0 // 16:c1 // 16], T.tk[:, s - 1, c0:c1], T.rl[:, s - 1, c0:c1], T.qs[:, c0:c1]
+            kd = ready(s, h) + ld["k"] + came["k"]
+            if ty[h] in "VW":
+                add("K" + n, "V", lambda: g.vector.tensor_tensor(tk, kw.indirect(offs), qq, A.subtract), kd + ["dq"])
+                if ty[h] == "V":
+                    add("R" + n, "V", lambda: g.vector.tensor_scalar(rl, tk, bbcol, 0.0, A.subtract, A.min), ["K" + n, "bb"])
+                else:
+                    add("R" + n, "S", lambda: g.scalar.activation(rl, tk, F.Relu, bias=bcol, scale=-1.0), ["K" + n, "db"])
+                return
+            j = apos.index("a" + n)
+            bank = banks[j % 3][:, 0:512]
+            held[h] = bank
+            free = []
+            if j >= 3:
+                w = apos[j - 3][1:]
+                z = TYPES[2 * int(w[0]) - 2 + (1 if w[1] == "B" else 0)] == "Z"
+                free = (["V6B1", "V6B2"] if w == "6B" else ["V" + w]) if z else ["R" + w]
+            add("K" + n, "S", gather("S", tk, kw, offs), kd)
+
+            def form():
+                g.tensor.matmul(bank, Id, qq, True, False)
+                return g.tensor.matmul(bank, nId, tk, False, True)
+            add("a" + n, "P", form, ["K" + n, "dq", "Id", "nId"] + free)
+            if ty[h] == "T":
+                add("R" + n, "V", lambda: g.vector.tensor_scalar(rl, bank, bcol, 0.0, A.add, A.max), ["a" + n, "db"])
+            else:
+                add("R" + n, "S", lambda: g.scalar.activation(bank if ty[h] == "Z" else rl, bank, F.Relu, bias=bcol), ["a" + n, "db"])
+
+        for h in ("F" if fk else "AB"):
+            keys(h)
+
+        def relus(h):
+            if fk:
+                return ["R%dF" % s]
+            return ["R%d%s" % (s, x) for x in ("AB" if h == "F" else h)]
+
+        vd = ld["v"] + came["v"]
+        fv = s < ND and GV[s - 1] and "Z" not in (ty["A"], ty["B"]) and (ty["A"] == "V") == (ty["B"] == "V")
+
+        def product(name, h, part):
+            c0, c1 = cols[part]
+            pr = T.pr[:, s - 1, c0:c1]
+            if h != "F" and ty[h] == "Z":
+                b0 = c0 - cols[h][0]
+                add(name, "V", lambda: g.vector.tensor_tensor(pr, T.vg[:, s - 1, c0:c1], held[h][:, b0:b0 + c1 - c0], A.mult),
+                    ["G%d%s" % (s, h)] + relus(h))
+            else:
+                add(name, "V", lambda: g.vector.tensor_tensor(pr, vw.indirect(T.off[:, s, c0 // 16:c1 // 16]), T.rl[:, s - 1, c0:c1], A.mult),
+                    vd + relus(h))
+
+        for h in ("F" if fv else "AB"):
+            n = "%d%s" % (s, h)
+            neg = ty["A" if h == "F" else h] == "V"
+            if h != "F" and ty[h] == "Z":
+                c0, c1 = cols[h]
+                add("G" + n, "S", gather("S", T.vg[:, s - 1, c0:c1], vw, T.off[:, s, c0 // 16:c1 // 16]), vd + ready(s, h))
+            if n == "6B":
+                product("V6B1", h, "B1")
+                product("V6B2", h, "B2")
+                sums["s6B1"] = (s, neg, ["B1"], "V6B1")
+                sums["last"] = neg
+            else:
+                product("V" + n, h, h)
+                sums["s" + n] = (s, neg, {"F": ["A", "B1", "B2"], "A": ["A"], "B": ["B1", "B2"]}[h], "V" + n)
+
+    for s in range(1, ND + 1):
+        level(s)
+
+    seq = {b: [n for n in ORDER if n in sums and b in sums[n][2]] for b in acc}
+    parts = {}
+    for n in ORDER:
+        if n in sums:
+            s, neg, bs, dep = sums[n]
+            parts[n] = []
+            for b in bs:
+                c0, c1 = cols[b]
+                add(n + "_" + b, "P",
+                    (lambda o, l, r, first, last: lambda: g.tensor.matmul(o, l, r, first, last))(
+                        acc[b], nId if neg else Id, T.pr[:, s - 1, c0:c1], seq[b][0] == n, seq[b][-1] == n),
+                    [dep, "Id", "nId"])
+                parts[n].append(n + "_" + b)
+    add("fA", "S", lambda: g.scalar.activation(T.yo[:, 0:512], acc["A"], F.Copy), [seq["A"][-1] + "_A"])
+    add("fB1", "S", lambda: g.scalar.activation(T.yo[:, 512:768], acc["B1"], F.Copy), [seq["B1"][-1] + "_B1"])
+    add("fB2", "V", lambda: g.vector.tensor_tensor(T.yo[:, 768:1024], acc["B2"], T.pr[:, ND - 1, 768:1024],
+                                                   A.subtract if sums["last"] else A.add), [seq["B2"][-1] + "_B2", "V6B2"])
+    dma("yA", "Y", T.y[:, 0:512], T.yo[:, 0:512], ["fA"])
+    dma("yB1", "S", T.y[:, 512:768], T.yo[:, 512:768], ["fB1"])
+    dma("yB2", "Y", T.y[:, 768:1024], T.yo[:, 768:1024], ["fB2"])
+    add("endY", "Y", None, ["yA", "yB2"])
+    add("endS", "S", None, ["yB1"])
+
+    order = list(pre)
+    for n in ORDER:
+        if n in parts:
+            order += parts[n]
+        elif n in ops:
+            order.append(n)
+            if n == "xk0":
+                order.append("dv2")
+    order += ["endY", "endS"]
+    assert sorted(order) == sorted(ops)
+
+    known = {q: set() for q in Q}
+    behind = {a: set() for a in arrive}
+    waits = {}
+    pos = {n: i for i, n in enumerate(order)}
+    for n in order:
+        q, fn, deps, inc = ops[n]
+        waits[n] = []
+        for d in sorted(set(deps), key=lambda x: -pos.get(x, -1)):
+            if d not in known[q]:
+                waits[n].append(d)
+                known[q] |= behind[d] | {d}
+        behind[n] = set(known[q])
+    waited = [n for n in order if any(n in w for w in waits.values())]
+    sem = {n: T.sem["s%d" % i] for i, n in enumerate(waited)}
+    for n in order:
+        q, fn, deps, inc = ops[n]
+        for d in waits[n]:
+            if d in arrive:
+                Q[q].wait_ge(T.sem[d], arrive[d])
+            else:
+                Q[q].wait_ge(sem[d], ops[d][3])
+        if fn is not None:
+            ins = fn()
+            if n in sem:
+                ins.then_inc(sem[n], inc)
+    if sent[0]:
+        g.wait_ge(T.sem.sent, sent[0])

@@ -1,10 +1,21 @@
+from concourse.bass import DstId, RemoteDMATransfer
 from concourse.mybir import AluOpType, ActivationFunctionType
 
 NT, NQ, NE, ND = 4096, 1024, 64, 6
 WIN = NT + NE * ND
 PW = NT + NE * (ND - 1)
-K1, V1 = 3072, 3072
-ZS = 1024
+TAIL_HI = NT + 3 * NE
+ROUND4 = 3.0 * 2 ** 24
+K1, V1 = 2560, 2048
+VDEP = ["xk0", "xk0"]
+KDEP = ""
+VLAST = ""
+VFIRST = ["", ""]
+LATEB = False
+ZN = 2
+ZS = 704
+XLAG = 0
+LB = 768
 
 SCRATCH = {
     "kwin": ("sbuf", [128, WIN], "bfloat16"), "vwin": ("sbuf", [128, WIN], "bfloat16"),
@@ -12,10 +23,12 @@ SCRATCH = {
     "parc": ("sbuf", [128, 256], "int32"), "hi": ("sbuf", [128, 256], "bfloat16"), "lo": ("sbuf", [128, 256], "bfloat16"),
     "upc": ("sbuf", [128, 64], "int32"), "exs": ("sbuf", [128, 4], "int32"), "exl": ("sbuf", [128, 4], "int32"),
     "off": ("sbuf", [128, 8, 72], "uint16"), "xla": ("sbuf", [128, 24], "uint16"), "xlb": ("sbuf", [128, 24], "uint16"),
-    "res": ("sbuf", [128, 6, 1088], "bfloat16"),
-    "cst": ("sbuf", [128, 400], "bfloat16"), "elo": ("sbuf", [128, 320], "bfloat16"),
+    "res": ("sbuf", [128, 6, 1088], "bfloat16"), "wf": ("sbuf", [128, 144], "float32"),
+    "sel": ("sbuf", [128, 144], "bfloat16"), "cst": ("sbuf", [128, 256], "bfloat16"), "ehi": ("sbuf", [128, 20], "bfloat16"),
     "qs": ("sbuf", [128, NQ], "bfloat16"), "bs": ("sbuf", [128, 8], "float32"), "bb": ("sbuf", [128, 8], "bfloat16"),
-    "tk": ("sbuf", [128, 6, NQ], "bfloat16"), "rl": ("sbuf", [128, 6, NQ], "bfloat16"), "vg": ("sbuf", [128, 6, NQ], "bfloat16"),
+    "nb": ("sbuf", [128, 8], "float32"),
+    "tk": ("sbuf", [128, 6, NQ], "bfloat16"), "rl": ("sbuf", [128, 6, NQ], "bfloat16"),
+    "fx": ("sbuf", [128, 6, NQ], "bfloat16"), "zz": ("sbuf", [128, NQ], "bfloat16"),
     "pr": ("sbuf", [128, 6, NQ], "float16"), "yo": ("sbuf", [128, NQ], "float32"),
     "xk": ("sbuf", [128, NE * ND], "bfloat16"), "xv": ("sbuf", [128, NE * ND], "bfloat16"),
     "accA": ("psum", [128, 512], "float32"), "accB1": ("psum", [128, 512], "float32"), "accB2": ("psum", [128, 512], "float32"),
@@ -23,21 +36,32 @@ SCRATCH = {
     "a0": ("psum", [128, 512], "float32"), "a1": ("psum", [128, 512], "float32"), "a2": ("psum", [128, 512], "float32"),
 }
 
-TYPES = "VTVTSZVSSSWZ"
-MODE = "HHHHA"
-GK = [1, 1, 1, 0, 1, 0]
-GV = [1, 0, 0, 1, 0, 0]
-XE = "SSSSSVSVVSSVS"
+TYPES = "VVVVSSVSSSSS"
+MODE = "HHHAA"
+CUT = 16
+GK = [1, 1, 2, 2, 1, 2]
+GR = [1, 1, 2, 2, 2, 2]
+GV = [1, 2, 1, 2, 2, 2]
+QE = False
+QN = ["VS"] * 6
+GQ = [[1, 1]] * 6
+XE = "SSSSSSSSSSSSS"
 KMSG = [[0], [1], [2], [3, 4, 5]]
 VMSG = [[0, 1, 2], [3, 4, 5]]
-ORDER = ("C1Bs C1As C1Bv P1B C1Av cpX cp1B P1A C2Bs C2Bv xk0 cp1A C2Av C2As P2B cp2B P2A C3Bv mk0 C3Bs cp2A xk1 P3B C3Av "
-         "mk1 cp3B C3As C4Bs C4Bv P3A cp3A P4B xk2 C4As xl02 C4Av P4A mk2 cp4B K1F C5Bs cp4A xv0 P5B R1F mv0 cp5B K2F C6Bv "
-         "P6B cp6B K3B xl35 R2F K3A xk3 a3B C5As R3B V1F G3B V2A V2B a3A V3B P5A xv3 cp5A mk3 K4A R3A K5A s1F s2A s2B s3B "
-         "a5A K4B a4B K6A mv3 R4A K5B K6B R5A R6A V3A V4A R4B V5A a5B a6B R6B V6A V4B s3A R5B s5A G6B s4A s6A V5B V6B2 s4B "
-         "s5B V6B1 fA fB2 yA yB2 s6B1 fB1 yB1").split()
+FE = "SSV"
+K1, GK, GR, GV, TYPES, CUT, KMSG, VMSG = 2048, [1, 1, 2, 2, 1, 2], [1, 1, 2, 2, 2, 2], [1, 1, 2, 2, 2, 2], "VVVVSSSSSSVS", 18, [[0], [1], [2], [3], [4, 5]], [[0, 1, 2], [3], [4, 5]]
+ORDER = "msc Id nId C1Av C1As cpX P1A C1Bv C1Bs bb xk0 P1B mk0 dv1 dv2 cp1A C2Av C2As P2A cp1B C2Bv C2Bs xk1 mk1 P2B cp2A C3Av C3As P3A cp2B C3Bv C3Bs xk2 P3B cp3A mk2 xl02 C4As cp3B K1F C4Bs P4A xv0 P4B xv3 mv0 cp4A xk3 R1F C5As cp4B mk3 mv3 K2F C5Bs K3B P5B R2F K3A P5A cp5B xl45 V1F xk4 a3A xv4 mk4 K4B mv4 a3B V2F R3A a4B K4A R3B V3A s1A s1B1 a4A R4B V3B K5F cp5A V4B K6A R4A s1B2 s2A s2B1 s2B2 s3A s3B1 s3B2 s4B1 s4B2 a5A R6A K6B V4A a5B V6A R5A a6B R5B V5A R6B V5B s4A s6A s5A fA V6B1 V6B2 yA s5B1 s5B2 s6B1 fB1 fB2 yB1 yB2".split()
+KDEP, K1, ZN, ZS, TYPES, GV = "l_ex", 2560, 1, 896, "VVVVVSSSSSVS", [1, 1, 2, 1, 2, 2]
+ORDER = "msc Id nId C1As C1Av P1A cpX C1Bv C1Bs cp1A xk0 C2Av P1B C2As mk0 dv1 dv2 P2A cp1B C2Bv C2Bs cp2A xk1 P2B C3Av C3As mk1 P3A cp2B C3Bv C3Bs xl02 xk2 cp3A P3B bb C4As mk2 cp3B K1F xk3 P4A C4Bs mk3 xv0 P4B cp4A K3B R1F mv0 cp4B K3A C5Bs a3B K2F K4B P5B R3B a4B cp5B xl45 R2F xk4 xv3 mk4 R3A C5As V3A xv4 P5A V1F K4A mv3 mv4 R4B s3A a4A V2F K5F cp5A V3B R4A s1A s1B1 s1B2 a5A K6B a5B K6A R5A s2A a6B R6A V6A R5B R6B V4F V5A V5B s2B1 s2B2 s3B1 s3B2 s6A s4A s4B1 s4B2 s5A fA V6B1 yA V6B2 s5B1 s5B2 s6B1 fB1 fB2 yB1 yB2".split()
+GK, GV, TYPES, MODE = [1, 1, 2, 2, 2, 2], [1, 2, 2, 1, 2, 2], "SVSSSSSVSSSZ", "HHHbb"
+ORDER = "msc Id nId C1As C1Av P1A cpX C1Bv C1Bs bb xk0 P1B cp1A mk0 dv1 C2Av C2As dv2 P2A cp1B C2Bv C2Bs xk1 P2B mk1 cp2A C3Av C3As P3A cp2B C3Bv C3Bs xl02 xk2 P3B xv0 mk2 cp3A C4As cp3B P4A C4Bv xk3 xv3 mk3 K1A mv0 mv3 K1B P4B K2F cp4A a1A cp4B R1B K3A C5Bv a2B R1A P5B K4B K4A R2B a2A cp5B xl45 R4B xk4 V4B a4A mk4 R2A C5As a3A V1A K3B P5A V2B xv4 R4A mv4 a3B cp5A V2A R3A K5A V4A K6A s4B1 s4B2 s1A s2B1 a5A V3A K5B a6A R5A V1B R3B V5A R6A s2B2 s2A s4A a5B K6B V6A R5B s3A a6B V3B G6B R6B V5B s1B1 s1B2 s5A s6A fA V6B1 V6B2 yA s3B1 s3B2 s5B1 s5B2 fB2 s6B1 fB1 yB2 yB1".split()
+LATEB, XLAG, K1, GK, GR, GV, TYPES, MODE = True, 1, 2048, [1, 1, 2, 1, 1, 2], [1, 2, 2, 2, 2, 2], [1, 1, 2, 1, 2, 2], "VVSSVSSSVSSS", "HHHHA"
+ORDER = "msc Id nId C1Bs C1As C1Bv P1B C1Av cp1B cpX C2Bv P1A xk0 C2Bs P2B mk0 dv1 dv2 bb cp1A C2Av C2As P2A cp2B C3Bv C3Bs P3B cp2A C3Av cp3B C4Bv xk1 C3As P3A C4Bs mk1 P4B xl02 cp3A xk2 xv0 C4As C4Av cp4B P4A K1F C5Bs P5B cp5B xk3 K2F C6B mk2 K3B mv0 R1F P6B a2A a2B K3A cp4A R3A cp6B xl45 V3A V1F mk3 a3B C5As P5A xk4 xv3 R2B R2A mk4 mv3 K4F cp5A V2F K5A xv4 R3B R5A V3B s3A s1A s1B1 s1B2 a4A a4B mv4 R4A R4B K6A V4F K5B s2A s2B1 s2B2 s3B1 s3B2 a6A a5B R6A V5A V6A K6B R5B V5B s4A s4B1 s4B2 s5A a6B R6B s6A fA V6B1 yA V6B2 s5B1 s5B2 s6B1 fB1 fB2 yB1 yB2".split()
+KDEP, VLAST, VDEP, GV, TYPES = "", "P1B", ["C2Bs", "C2Bs"], [1, 1, 1, 1, 2, 2], "VSVSVSSSVSSS"
+ORDER = "msc Id nId C1Bs C1Bv C1As C1Av P1B cpX xk0 P1A mk0 cp1B C2Bv C2Bs dv1 dv2 cp1A P2B C2Av C2As P2A cp2B C3Bv C3Bs bb xk1 cp2A C3Av P3B C3As mk1 P3A cp3B C4Bv xk2 C4Bs mk2 xl02 K1A K1B P4B cp3A xv0 C4Av a1B C4As mv0 cp4B K2A C5Bs P4A K3A K2B P5B R2A R1B cp4A cp5B R1A C6B V1A xk3 P6B C5As mk3 R3A a2B K3B cp6B xl45 V3A P5A xk4 xv3 mk4 R2B V1B a3B xv4 K4F V2A mv3 mv4 cp5A V2B R3B s1A s3A s1B1 s1B2 s2A a4B K5A K6A a4A R5A R4B V3B s2B1 s2B2 a6A R4A V5A K5B V4F R6A s3B1 s3B2 s5A a5B K6B V6A R5B a6B V5B R6B V6B1 s4A s4B1 s4B2 s6A fA V6B2 yA s5B1 s5B2 fB2 s6B1 fB1 yB2 yB1".split()
+HOOK = None
 
-ARR = ["a_ex"] + ["a_k%d" % m[0] for m in KMSG] + ["a_v%d" % m[0] for m in VMSG]
-SEMAPHORES = ["sent"] + ARR + ["s%d" % i for i in range(149 - len(ARR))]
+SEMAPHORES = ["s%d" % i for i in range(149)] + ["sent"]
 
 
 def rank_program(g, core, T, topo):
@@ -52,23 +76,49 @@ def rank_program(g, core, T, topo):
     ops = {}
 
     def add(name, q, fn, deps, inc=1):
-        ops[name] = (q, fn, list(deps), inc)
+        ops[name] = [q, fn, list(deps), inc]
 
     def dma(name, q, out, in_, deps):
         add(name, q, lambda: Q[q].dma_start(out, in_), deps, 16)
 
     sent = [0]
+    landed = ["a_ex"] + ["a_k%d" % m[0] for m in KMSG] + ["a_v%d" % m[0] for m in VMSG]
+    for s in range(1, ND + 1):
+        for h in ("F" if TYPES[2 * s - 2:2 * s] == "XX" and GR[s - 1] == 1 else "AB"):
+            if TYPES[2 * s - 2 + (h == "B")] == "X":
+                landed += ["a_e%d%s" % (s, h), "a_h%d%s" % (s, h)]
+    landed += [d for d in [KDEP] + VDEP if d.startswith("l_")]
+    sem = {n: T.sem["s%d" % i] for i, n in enumerate(landed)}
+    kdep = [KDEP] if takes and KDEP else []
+    vdep = [([d] if gives else [VLAST]) if takes and d and (gives or VLAST) else [] for d in VDEP]
+    if not takes:
+        vdep = [[d] if d else [] for d in VFIRST]
+    held = kdep + vdep[0] + vdep[1]
 
-    def send(name, dst, out, in_, sem, deps):
+    def send(name, dst, out, in_, deps):
         rid, pid = topo.addr(dst)[0:2]
-        sent[0] += len(topo.engines(core, dst))
-        add(name, "G", lambda: g.remote_dma(out, in_, T.sem[sem], T.sem.sent, pid, rid, topo.mask(core, dst)), deps, 0)
+        if "l_" + name in held:
+            arrive["l_" + name], left = len(topo.engines(core, dst)), sem["l_" + name]
+        else:
+            sent[0] += len(topo.engines(core, dst))
+            left = T.sem.sent
+        add("m" + name, "G", lambda: g.remote_dma(out, in_, sem["a_" + name], left, pid, rid, topo.mask(core, dst)), deps, 0)
+
+    twin = [c for c in T.cores if c != core and topo.chip(c) == topo.chip(core)][0]
+
+    def fold(name, out, srcs, op, deps):
+        rid, pid = topo.addr(twin)[0:2]
+        sent[0] += len(topo.engines(core, twin))
+        arrive["a_" + name] = len(topo.engines(twin, core))
+        add("m" + name, "G", lambda: g.remote_dma_fused(
+            [RemoteDMATransfer(dst_ids=[DstId(rid=rid, pnc=pid)], dma_engine_mask=topo.mask(core, twin), remote_sem=sem["a_" + name],
+                               srcs=srcs, dsts=[out], alu_op=op)], local_sem=T.sem.sent), deps, 0)
 
     arrive = {}
     if gives:
         arrive["a_ex"] = len(topo.engines(T.cores[rank + 1], core))
     if takes:
-        for a in ARR[1:]:
+        for a in ["a_k%d" % m[0] for m in KMSG] + ["a_v%d" % m[0] for m in VMSG]:
             arrive[a] = len(topo.engines(T.cores[rank - 1], core))
 
     def gather(e, out, win, offs):
@@ -76,46 +126,61 @@ def rank_program(g, core, T, topo):
             return lambda: g.vector.tensor_copy(out, win.indirect(offs))
         return lambda: g.scalar.activation(out, win.indirect(offs), F.Copy)
 
-    Wm, Id, nId = T.cst[:, 0:144], T.cst[:, 144:272], T.cst[:, 272:400]
+    Id, nId = T.cst[:, 0:128], T.cst[:, 128:256]
 
     if takes:
         dma("dex", "S", T.exs[:], T.ex[:], [])
     dma("dpar", "Y", T.parc[:], T.par[:], [])
     dma("dup", "S", T.upc[:], T.up[:], [])
+    if QE:
+        dma("db", "S", T.bs[:, 0:ND], T.b[:], [])
+        dma("dq", "Y", T.qs[:], T.q[:], [])
     dma("dk1", "Y", T.kwin[:, 0:K1], T.k[:, 0:K1], [])
-    dma("db", "S", T.bs[:, 0:ND], T.b[:], [])
     add("ms0", "V", lambda: g.vector.memset(T.pwin[:, 0:ZS], 0.0), [])
-    add("ms", "V", lambda: g.vector.memset(T.pwin[:, ZS:NT - ZS], 0.0), [])
-    add("mss", "S", lambda: g.scalar.activation(T.pwin[:, NT - ZS:NT], T.pwin[:, 0:ZS], F.Copy), ["ms0"])
     win = ["dhi", "dlo"]
     if takes:
-        add("io1", "G", lambda: g.iota(T.pwin[:, NT:PW], [[NE, ND - 1], [0, NE]], NT + NE, 0, allow_small_or_imprecise_dtypes=True), [])
-        add("io2", "G", lambda: g.iota(T.elo[:], [[0, ND - 1], [1, NE]], 0, 0, allow_small_or_imprecise_dtypes=True), [])
-        dma("delo", "S", T.pwin[1:128:16, NT:PW], T.elo[0:8, :], ["io1", "io2"])
-        send("mex", T.cores[rank - 1], T.exl[:], T.exs[:], "a_ex", ["dex"])
-        win.append("delo")
+        add("mse", "V", lambda: g.vector.memset(T.ehi[:], float(TAIL_HI)), [])
+        add("io", "G", lambda: g.iota(T.pwin[:, NT:PW], [[1, PW - NT]], NT + NE - TAIL_HI, 0, allow_small_or_imprecise_dtypes=True), [])
+        win.append("dehi")
+    add("ms", "V", lambda: g.vector.memset(T.pwin[:, ZS:NT - ZN * ZS], 0.0), [])
+    clear = ["ms", "mss"]
+    if ZN == 2:
+        add("mss0", "S", lambda: g.scalar.activation(T.pwin[:, NT - 2 * ZS:NT - ZS], T.pwin[:, 0:ZS], F.Copy), ["ms0"])
+        clear.append("mss0")
+    else:
+        add("mss", "S", lambda: g.scalar.activation(T.pwin[:, NT - ZS:NT], T.pwin[:, 0:ZS], F.Copy), ["ms0"])
+    add("iw", "G", lambda: g.iota(T.wf[:], [[-32, 9], [-2000, 16]], 31, 2, allow_small_or_imprecise_dtypes=True), [])
+    if takes:
+        dma("dehi", "Y" if LATEB else "S", T.pwin[0:128:16, NT:PW], T.ehi[:], ["io", "mse"])
+        send("ex", T.cores[rank - 1], T.exl[:], T.exs[:], ["dex"])
+    if ZN == 2:
+        add("mss", "S", lambda: g.scalar.activation(T.pwin[:, NT - ZS:NT], T.pwin[:, 0:ZS], F.Copy), ["ms0"])
+    if not QE and not LATEB:
+        dma("db", "S", T.bs[:, 0:ND], T.b[:], [])
     add("hi", "V", lambda: g.vector.tensor_copy(T.hi[:], T.parc[:]), ["dpar"])
-    dma("dhi", "Y", T.pwin[0:128:16, 0:NT], T.hi[:], ["hi", "ms", "mss"])
+    dma("dhi", "Y", T.pwin[0:128:16, 0:NT], T.hi[:], ["hi"] + clear)
     add("lo", "V", lambda: g.vector.tensor_tensor(T.lo[:], T.parc[:], T.hi[:], A.subtract), ["hi"])
-    dma("dlo", "S", T.pwin[1:128:16, 0:NT], T.lo[:], ["lo", "ms", "mss"])
-    dma("dk2", "Y", T.kwin[:, K1:NT], T.k[:, K1:NT], [])
-    dma("dq", "Y", T.qs[:], T.q[:], [])
-    add("msc", "V", lambda: g.vector.memset(T.cst[:], 0.0), [])
+    dma("dlo", "Y", T.pwin[1:128:16, 0:NT], T.lo[:], ["lo"] + clear)
+    if K1 < NT:
+        dma("dk2", "Y", T.kwin[:, K1:NT], T.k[:, K1:NT], kdep)
+    if not QE:
+        dma("dq", "Y", T.qs[:], T.q[:], kdep)
+        if LATEB:
+            dma("db", "Y", T.bs[:, 0:ND], T.b[:], [])
+    add("W", "V", lambda: g.vector.tensor_scalar(T.sel[:], T.wf[:], ROUND4, ROUND4, A.add, A.is_equal), ["iw"])
     add("cpU", "V", lambda: g.vector.tensor_copy(T.off[:, 1, 0:64], T.upc[:]), ["dup"])
+    pre = list(ops)
+    add("msc", "V", lambda: g.vector.memset(T.cst[:], 0.0), [])
+    if "X" in TYPES:
+        add("msz", "V", lambda: g.vector.memset(T.zz[:], 0.0), [])
     add("bb", "V", lambda: g.vector.tensor_copy(T.bb[:, 0:ND], T.bs[:, 0:ND]), ["db"])
-    add("W1", "G", lambda: g.affine_select(Wm, Wm, [[-16, 9], [-1000, 16]], A.not_equal, 1.0, 16, 1), ["msc"])
-    add("W2", "G", lambda: g.affine_select(Wm, Wm, [[-16, 9], [-1000, 16]], A.not_equal, 1.0, 15, 1), ["W1"])
+    if "M" in TYPES:
+        add("nb", "S", lambda: g.scalar.activation(T.nb[:, 0:ND], T.bs[:, 0:ND], F.Copy, scale=-1.0), ["db"])
     add("Id", "G", lambda: g.affine_select(Id, Id, [[-1, 128]], A.not_equal, 1.0, 0, 1), ["msc"])
     add("nId", "G", lambda: g.affine_select(nId, nId, [[-1, 128]], A.not_equal, -1.0, 0, 1), ["msc"])
-    if gives:
-        dma("dv1", "Y", T.vwin[:, 0:V1], T.v[:, 0:V1], ["dhi", "dlo"])
-        pre = list(ops)
-        dma("dv2", "Y", T.vwin[:, V1:NT], T.v[:, V1:NT], ["xk0"])
-        ld = {"k": ["dk1", "dk2"], "v": ["dv1", "dv2"]}
-    else:
-        dma("dv1", "Y", T.vwin[:, 0:NT], T.v[:], ["dhi", "dlo"])
-        pre = list(ops)
-        ld = {"k": ["dk1", "dk2"], "v": ["dv1"]}
+    for j, (a, b) in enumerate(((0, V1), (V1, NT))):
+        dma("dv%d" % (j + 1), "Y", T.vwin[:, a:b], T.v[:, a:b], vdep[j])
+    ld = {"k": ["dk1", "dk2"][0:1 + (K1 < NT)], "v": ["dv1", "dv2"]}
 
     def ready(s, h):
         if s == 1:
@@ -127,7 +192,7 @@ def rank_program(g, core, T, topo):
         return ["cp%d%s" % (s - 1, x) for x in ("AB" if h == "F" else h)]
 
     def xready(t):
-        return ["cpX"] if t == 0 else ready(t + 2, "B")
+        return ["cpX"] if t == 0 else ready(t + 1 + XLAG, "B")
 
     pwin = T.pwin[:, 0:(PW if takes else NT)]
 
@@ -136,28 +201,28 @@ def rank_program(g, core, T, topo):
 
         def emit():
             for i in range(16):
-                ins = g.tensor.matmul(ps[:, 0:n], T.cst[:, 16 - i:144 - i], T.res[:, s - 1, r0 + i:r0 + 16 * n:16], i == 0, i == 15)
+                ins = g.tensor.matmul(ps[:, 0:n], T.sel[:, 16 - i:144 - i], T.res[:, s - 1, r0 + i:r0 + 16 * n:16], i == 0, i == 15)
             return ins
-        add("P" + name, "P", emit, deps + ["W2"])
+        add("P" + name, "P", emit, deps + ["W"])
         add("cp" + name, "V", lambda: g.vector.tensor_copy(T.off[:, s + 1, c0:c1], ps[:, 0:n]), ["P" + name])
 
     if gives:
-        add("cpX", "V", lambda: g.vector.tensor_copy(T.off[:, 2, 64:68], T.exl[:]), ["a_ex"])
+        add("cpX", "V", lambda: g.vector.tensor_copy(T.off[:, 1 + XLAG, 64:68], T.exl[:]), ["a_ex"])
     for s in range(1, ND):
         m = MODE[s - 1]
-        end = 68 if (s > 1 and gives) else 64
+        end = 68 if (s > XLAG and gives) else 64
         for h in ("F" if m in "FSV" else "AB"):
             c0, c1 = {"F": (0, end), "A": (0, 32), "B": (32, end)}[h]
-            d = ready(s, h) + win + (["cpX"] if s == 2 and h != "A" and gives else [])
-            es = {"H": "vs", "F": "vs", "S": "s", "A": "s", "V": "v", "B": "v" if h == "A" else "s"}[m]
-            cuts = [c0, c1] if len(es) == 1 else [c0, (c0 + c1) // 2, c1]
+            d = ready(s, h) + win + (["cpX"] if s == 1 + XLAG and h != "A" and gives else [])
+            es = {"H": "vs", "F": "vs", "S": "s", "A": "s", "V": "v", "W": "v", "B": "v" if h == "A" else "s", "b": "s" if h == "A" else "v"}[m]
+            cuts = [c0, c1] if len(es) == 1 else [c0, c0 + CUT * (2 if h == "F" else 1), c1]
             for j, e in enumerate(es):
                 a, b = cuts[j], cuts[j + 1]
                 add("C%d%s%s" % (s, h, e), e.upper(), gather(e.upper(), T.res[:, s - 1, 16 * a:16 * b], pwin, T.off[:, s, a:b]), d)
             relay("%d%s" % (s, h), s, c0, c1, 16 * c0, T.chB if h == "B" else T.chA, ["C%d%s%s" % (s, h, e) for e in es])
-    if gives:
-        add("C6Bv", XE[12], gather(XE[12], T.res[:, 5, 0:64], pwin, T.off[:, 6, 64:68]), ready(6, "B"))
-        relay("6B", 6, 64, 68, 0, T.chB, ["C6Bv"])
+    if gives and XLAG:
+        add("C6B", XE[12], gather(XE[12], T.res[:, 5, 0:64], pwin, T.off[:, 6, 64:68]), ready(6, "B"))
+        relay("6B", 6, 64, 68, 0, T.chB, ["C6B"])
 
     arr = {"k": {}, "v": {}}
     lists = {}
@@ -173,134 +238,180 @@ def rank_program(g, core, T, topo):
                 if key not in lists:
                     xl = (T.xla if nm == "k" else T.xlb)[:, 4 * a:4 * b]
                     lists[key] = xl
-                    add(key, "V", (lambda o, i: lambda: g.vector.tensor_copy(o, i))(xl, T.off[:, a + 2:b + 2, 64:68]),
+                    add(key, "V", (lambda o, i: lambda: g.vector.tensor_copy(o, i))(xl, T.off[:, a + 1 + XLAG:b + 1 + XLAG, 64:68]),
                         sum([xready(t) for t in m], []))
                 d, offs = [key], lists[key]
             else:
-                d, offs = xready(a), T.off[:, a + 2, 64:68]
+                d, offs = xready(a), T.off[:, a + 1 + XLAG, 64:68]
             e = XE[a + (6 if nm == "v" else 0)]
             add("x%s%d" % (nm, a), e, gather(e, st[:, NE * a:NE * b], wn[:, 0:NT], offs), d + ld[nm])
-            send("m%s%d" % (nm, a), T.cores[rank + 1], wn[:, NT + NE * a:NT + NE * b], st[:, NE * a:NE * b],
-                 "a_%s%d" % (nm, a), ["x%s%d" % (nm, a)])
+            send("%s%d" % (nm, a), T.cores[rank + 1], wn[:, NT + NE * a:NT + NE * b], st[:, NE * a:NE * b], ["x%s%d" % (nm, a)])
 
-    apos = [n for n in ORDER if n[0] == "a"]
-    banks = [T.a0, T.a1, T.a2]
-    cols = {"F": (0, 1024), "A": (0, 512), "B": (512, 1024), "B1": (512, 768), "B2": (768, 1024)}
-    acc = {"A": T.accA[:, 0:512], "B1": T.accB1[:, 0:256], "B2": T.accB2[:, 0:256]}
+    banks = [T.a0[:, 0:512], T.a1[:, 0:512], T.a2[:, 0:512]]
+    bank = {}
+    cols = {"F": (0, 1024), "A": (0, 512), "B": (512, 1024), "B1": (512, LB), "B2": (LB, 1024),
+            "a": (0, 256), "b": (256, 512), "c": (512, 768), "d": (768, 1024)}
+    acc = {"A": T.accA[:, 0:512], "B1": T.accB1[:, 0:LB - 512], "B2": T.accB2[:, 0:1024 - LB]}
+    fe = dict(zip(("A", "B1", "B2"), FE))
     sums = {}
+    ends = {}
 
     def level(s):
-        fk = GK[s - 1] and TYPES[2 * s - 2] in "VW"
-        ty = {h: TYPES[2 * s - 2 + (1 if h == "B" and not fk else 0)] for h in "ABF"}
+        ty = {"A": TYPES[2 * s - 2], "B": TYPES[2 * s - 1]}
+        same = ty["A"] == ty["B"]
         wcols = NT + NE * s if takes else NT
         kw, vw = T.kwin[:, 0:wcols], T.vwin[:, 0:wcols]
         came = {x: (sorted(set(arr[x][i] for i in range(s))) if takes else []) for x in "kv"}
         bcol, bbcol = T.bs[:, s - 1:s], T.bb[:, s - 1:s]
-        held = {}
-
-        def keys(h):
-            n = "%d%s" % (s, h)
-            c0, c1 = cols[h]
-            offs, tk, rl, qq = T.off[:, s, c0 // 16:c1 // 16], T.tk[:, s - 1, c0:c1], T.rl[:, s - 1, c0:c1], T.qs[:, c0:c1]
-            kd = ready(s, h) + ld["k"] + came["k"]
-            if ty[h] in "VW":
-                add("K" + n, "V", lambda: g.vector.tensor_tensor(tk, kw.indirect(offs), qq, A.subtract), kd + ["dq"])
-                if ty[h] == "V":
-                    add("R" + n, "V", lambda: g.vector.tensor_scalar(rl, tk, bbcol, 0.0, A.subtract, A.min), ["K" + n, "bb"])
-                else:
-                    add("R" + n, "S", lambda: g.scalar.activation(rl, tk, F.Relu, bias=bcol, scale=-1.0), ["K" + n, "db"])
-                return
-            j = apos.index("a" + n)
-            bank = banks[j % 3][:, 0:512]
-            held[h] = bank
-            free = []
-            if j >= 3:
-                w = apos[j - 3][1:]
-                z = TYPES[2 * int(w[0]) - 2 + (1 if w[1] == "B" else 0)] == "Z"
-                free = (["V6B1", "V6B2"] if w == "6B" else ["V" + w]) if z else ["R" + w]
-            add("K" + n, "S", gather("S", tk, kw, offs), kd)
-
-            def form():
-                g.tensor.matmul(bank, Id, qq, True, False)
-                return g.tensor.matmul(bank, nId, tk, False, True)
-            add("a" + n, "P", form, ["K" + n, "dq", "Id", "nId"] + free)
-            if ty[h] == "T":
-                add("R" + n, "V", lambda: g.vector.tensor_scalar(rl, bank, bcol, 0.0, A.add, A.max), ["a" + n, "db"])
-            else:
-                add("R" + n, "S", lambda: g.scalar.activation(bank if ty[h] == "Z" else rl, bank, F.Relu, bias=bcol), ["a" + n, "db"])
-
-        for h in ("F" if fk else "AB"):
-            keys(h)
-
-        def relus(h):
-            if fk:
-                return ["R%dF" % s]
-            return ["R%d%s" % (s, x) for x in ("AB" if h == "F" else h)]
-
         vd = ld["v"] + came["v"]
-        fv = s < ND and GV[s - 1] and "Z" not in (ty["A"], ty["B"]) and (ty["A"] == "V") == (ty["B"] == "V")
+        made = {"K": {}, "R": {}, "Q": {}, "N": {}}
 
-        def product(name, h, part):
+        def half(part):
+            return "A" if cols[part][0] < 512 else "B"
+
+        def over(kind, part):
+            return [n for x, n in made[kind].items() if cols[x][0] < cols[part][1] and cols[part][0] < cols[x][1]]
+
+        def keys(part):
+            n, t = "K%d%s" % (s, part), ty[half(part)]
             c0, c1 = cols[part]
-            pr = T.pr[:, s - 1, c0:c1]
-            if h != "F" and ty[h] == "Z":
-                b0 = c0 - cols[h][0]
-                add(name, "V", lambda: g.vector.tensor_tensor(pr, T.vg[:, s - 1, c0:c1], held[h][:, b0:b0 + c1 - c0], A.mult),
-                    ["G%d%s" % (s, h)] + relus(h))
+            offs, tk, qq = T.off[:, s, c0 // 16:c1 // 16], T.tk[:, s - 1, c0:c1], T.qs[:, c0:c1]
+            kd = ready(s, "F" if part == "F" else half(part)) + ld["k"] + came["k"]
+            if t == "M":
+                add(n, "V", lambda: g.vector.tensor_tensor(tk, kw.indirect(offs), T.rl[:, s - 1, c0:c1], A.min), kd + over("Q", part))
+            elif t in "VW":
+                add(n, "V", lambda: g.vector.tensor_tensor(tk, kw.indirect(offs), qq, A.subtract), kd + ["dq"])
+            elif t in "DU":
+                add(n, "S", lambda: g.scalar.activation(tk, kw.indirect(offs), F.Copy, scale=-1.0), kd)
+            elif t == "X":
+                add(n, "S", lambda: g.scalar.activation(tk, kw.indirect(offs), F.Identity, bias=bcol, scale=-1.0), kd + ["db"])
             else:
-                add(name, "V", lambda: g.vector.tensor_tensor(pr, vw.indirect(T.off[:, s, c0 // 16:c1 // 16]), T.rl[:, s - 1, c0:c1], A.mult),
-                    vd + relus(h))
+                add(n, "S", gather("S", tk, kw, offs), kd)
+            made["K"][part] = n
 
-        for h in ("F" if fv else "AB"):
-            n = "%d%s" % (s, h)
-            neg = ty["A" if h == "F" else h] == "V"
-            if h != "F" and ty[h] == "Z":
-                c0, c1 = cols[h]
-                add("G" + n, "S", gather("S", T.vg[:, s - 1, c0:c1], vw, T.off[:, s, c0 // 16:c1 // 16]), vd + ready(s, h))
-            if n == "6B":
-                product("V6B1", h, "B1")
-                product("V6B2", h, "B2")
-                sums["s6B1"] = (s, neg, ["B1"], "V6B1")
-                sums["last"] = neg
+        def relu(part):
+            n, t = "%d%s" % (s, part), ty[half(part)]
+            c0, c1 = cols[part]
+            tk, rl, qq = T.tk[:, s - 1, c0:c1], T.rl[:, s - 1, c0:c1], T.qs[:, c0:c1]
+            made["R"][part] = "R" + n
+            if t == "V":
+                add("R" + n, "V", lambda: g.vector.tensor_scalar(rl, tk, bbcol, 0.0, A.subtract, A.min), over("K", part) + ["bb"])
+            elif t == "W":
+                add("R" + n, "S", lambda: g.scalar.activation(rl, tk, F.Relu, bias=bcol, scale=-1.0), over("K", part) + ["db"])
+            elif t in "DU":
+                add("d" + n, "G", lambda: g.dma_start(tk, qq, accum_op=A.add), over("K", part) + ["dq"], 16)
+                if t == "D":
+                    add("R" + n, "V", lambda: g.vector.tensor_scalar(rl, tk, bbcol, 0.0, A.add, A.max), ["d" + n, "bb"])
+                else:
+                    add("R" + n, "S", lambda: g.scalar.activation(rl, tk, F.Relu, bias=bcol), ["d" + n, "db"])
+            elif t == "M":
+                add("d" + n, "G", lambda: g.dma_start(tk, T.fx[:, s - 1, c0:c1], accum_op=A.add), over("K", part) + over("N", part), 16)
+                made["R"][part] = "d" + n
+            elif t == "X":
+                fx = T.fx[:, s - 1, c0:c1]
+                fold("e" + n, fx, [tk, qq], 1, over("K", part) + ["dq"])
+                fold("h" + n, rl, [fx, T.zz[:, c0:c1]], 2, ["a_e" + n, "msz"])
+                made["R"][part] = "a_h" + n
             else:
-                product("V" + n, h, h)
-                sums["s" + n] = (s, neg, {"F": ["A", "B1", "B2"], "A": ["A"], "B": ["B1", "B2"]}[h], "V" + n)
+                def emit():
+                    g.tensor.matmul(bank[n], Id, qq, True, False)
+                    return g.tensor.matmul(bank[n], nId, tk, False, True)
+                add("a" + n, "P", emit, over("K", part) + ["dq", "Id", "nId"])
+                if t == "T":
+                    add("R" + n, "V", lambda: g.vector.tensor_scalar(rl, bank[n], bcol, 0.0, A.add, A.max), ["a" + n, "db"])
+                else:
+                    add("R" + n, "S", lambda: g.scalar.activation(bank[n] if t == "Z" else rl, bank[n], F.Relu, bias=bcol), ["a" + n, "db"])
+                if t == "Z":
+                    add("G" + n, "S", gather("S", rl, vw, T.off[:, s, c0 // 16:c1 // 16]), ready(s, part) + vd)
+
+        def ahead(kind, part, e):
+            c0, c1 = cols[part]
+            n, qq = "%s%d%s" % (kind, s, part), T.qs[:, c0:c1]
+            out, sign = (T.rl[:, s - 1, c0:c1], 1.0) if kind == "Q" else (T.fx[:, s - 1, c0:c1], -1.0)
+            if e == "V":
+                add(n, "V", lambda: g.vector.tensor_scalar(out, qq, bbcol, sign, A.add, A.mult), ["dq", "bb"])
+            elif kind == "Q":
+                add(n, "S", lambda: g.scalar.activation(out, qq, F.Identity, bias=bcol), ["dq", "db"])
+            else:
+                add(n, "S", lambda: g.scalar.activation(out, qq, F.Identity, bias=T.nb[:, s - 1:s], scale=-1.0), ["dq", "nb"])
+            made[kind][part] = n
+
+        for kind, e, n in zip("QN", QN[s - 1], GQ[s - 1]):
+            for part in {1: "F" if same else "AB", 2: "AB", 4: "abcd"}[n]:
+                if ty[half(part)] == "M":
+                    ahead(kind, part, e)
+        for part in {1: "F" if same else "AB", 2: "AB", 4: "abcd"}[GK[s - 1]]:
+            keys(part)
+        for part in ("F" if same and GR[s - 1] == 1 and ty["A"] in "VWDUXM" else "AB"):
+            relu(part)
+        fv = s < ND and GV[s - 1] == 1 and len({(t in "VM", t == "M") for t in ty.values()}) == 1 and "Z" not in ty.values()
+
+        def product(part):
+            c0, c1 = cols[part]
+            name, h = "V%d%s" % (s, part), half(part)
+            pr, rl, n = T.pr[:, s - 1, c0:c1], (T.tk if ty[h] == "M" else T.rl)[:, s - 1, c0:c1], "%d%s" % (s, h)
+            if ty[h] == "Z":
+                b0 = c0 - cols[h][0]
+                add(name, "V", lambda: g.vector.tensor_tensor(pr, rl, bank[n][:, b0:b0 + c1 - c0], A.mult), ["G" + n, "R" + n])
+            else:
+                add(name, "V", lambda: g.vector.tensor_tensor(pr, vw.indirect(T.off[:, s, c0 // 16:c1 // 16]), rl, A.mult),
+                    vd + over("R", part))
+            neg = ty[h] in "VM"
+            for b in {"F": ["A", "B1", "B2"], "B": ["B1", "B2"]}.get(part, [part]):
+                if s == ND and fe[b] == "V":
+                    sums["last" + b] = (name, neg)
+                else:
+                    add_sum("s%d%s" % (s, b), b, neg, name)
+
+        def add_sum(n, b, neg, dep):
+            c0, c1 = cols[b]
+            add(n, "P", lambda: g.tensor.matmul(acc[b], nId if neg else Id, T.pr[:, s - 1, c0:c1], ends[n][0], ends[n][1]), [dep, "Id", "nId"])
+            sums.setdefault(b, []).append(n)
+
+        for part in ("F" if fv else ("A", "B") if s < ND else ("A", "B1", "B2")):
+            product(part)
 
     for s in range(1, ND + 1):
         level(s)
 
-    seq = {b: [n for n in ORDER if n in sums and b in sums[n][2]] for b in acc}
-    parts = {}
-    for n in ORDER:
-        if n in sums:
-            s, neg, bs, dep = sums[n]
-            parts[n] = []
-            for b in bs:
-                c0, c1 = cols[b]
-                add(n + "_" + b, "P",
-                    (lambda o, l, r, first, last: lambda: g.tensor.matmul(o, l, r, first, last))(
-                        acc[b], nId if neg else Id, T.pr[:, s - 1, c0:c1], seq[b][0] == n, seq[b][-1] == n),
-                    [dep, "Id", "nId"])
-                parts[n].append(n + "_" + b)
-    add("fA", "S", lambda: g.scalar.activation(T.yo[:, 0:512], acc["A"], F.Copy), [seq["A"][-1] + "_A"])
-    add("fB1", "S", lambda: g.scalar.activation(T.yo[:, 512:768], acc["B1"], F.Copy), [seq["B1"][-1] + "_B1"])
-    add("fB2", "V", lambda: g.vector.tensor_tensor(T.yo[:, 768:1024], acc["B2"], T.pr[:, ND - 1, 768:1024],
-                                                   A.subtract if sums["last"] else A.add), [seq["B2"][-1] + "_B2", "V6B2"])
-    dma("yA", "Y", T.y[:, 0:512], T.yo[:, 0:512], ["fA"])
-    dma("yB1", "S", T.y[:, 512:768], T.yo[:, 512:768], ["fB1"])
-    dma("yB2", "Y", T.y[:, 768:1024], T.yo[:, 768:1024], ["fB2"])
-    add("endY", "Y", None, ["yA", "yB2"])
-    add("endS", "S", None, ["yB1"])
+    def empty(b, q):
+        c0, c1 = cols[b]
+        if fe[b] == "V":
+            name, neg = sums["last" + b]
+            add("f" + b, "V", lambda: g.vector.tensor_tensor(T.yo[:, c0:c1], acc[b], T.pr[:, ND - 1, c0:c1],
+                                                             A.subtract if neg else A.add), sums[b] + [name])
+        else:
+            add("f" + b, "S", lambda: g.scalar.activation(T.yo[:, c0:c1], acc[b], F.Copy), sums[b])
+        dma("y" + b, q, T.y[:, c0:c1], T.yo[:, c0:c1], ["f" + b])
 
-    order = list(pre)
-    for n in ORDER:
-        if n in parts:
-            order += parts[n]
-        elif n in ops:
-            order.append(n)
-            if n == "xk0":
-                order.append("dv2")
-    order += ["endY", "endS"]
+    empty("A", "Y")
+    empty("B1", "S" if fe["B1"] == "S" else "Y")
+    empty("B2", "Y")
+
+    if HOOK is not None:
+        for n in ops:
+            if n[0] == "a":
+                bank[n[1:]] = banks[0]
+            if n[0] == "s":
+                ends[n] = (True, True)
+        HOOK[rank] = (ops, pre, arrive)
+        return
+
+    order = pre + [n for n in ORDER if n in ops]
+    forms = [n for n in order if n[0] == "a"]
+    for j, n in enumerate(forms):
+        bank[n[1:]] = banks[j % 3]
+        if j >= 3:
+            w = forms[j - 3][1:]
+            ops[n][2].extend([x for x in ops if x.startswith("V" + w)] if "G" + w in ops else ["R" + w])
+    for b in acc:
+        seq = [n for n in order if n in sums[b]]
+        for n in seq:
+            ends[n] = (n == seq[0], n == seq[-1])
+        ops["f" + b][2] = [d for d in ops["f" + b][2] if d not in seq[:-1]]
+    for q in "YS":
+        add("end" + q, q, None, [n for n in order if n[0] == "y" and ops[n][0] == q])
+        order.append("end" + q)
     assert sorted(order) == sorted(ops)
 
     known = {q: set() for q in Q}
@@ -316,17 +427,15 @@ def rank_program(g, core, T, topo):
                 known[q] |= behind[d] | {d}
         behind[n] = set(known[q])
     waited = [n for n in order if any(n in w for w in waits.values())]
-    sem = {n: T.sem["s%d" % i] for i, n in enumerate(waited)}
+    for i, n in enumerate(waited):
+        sem[n] = T.sem["s%d" % (len(landed) + i)]
     for n in order:
         q, fn, deps, inc = ops[n]
         for d in waits[n]:
-            if d in arrive:
-                Q[q].wait_ge(T.sem[d], arrive[d])
-            else:
-                Q[q].wait_ge(sem[d], ops[d][3])
+            Q[q].wait_ge(sem[d], arrive[d] if d in arrive else ops[d][3])
         if fn is not None:
             ins = fn()
-            if n in sem:
+            if n in waited:
                 ins.then_inc(sem[n], inc)
     if sent[0]:
         g.wait_ge(T.sem.sent, sent[0])

from concourse.bass import DstId, RemoteDMATransfer
from concourse.mybir import AluOpType, ActivationFunctionType

NT, NQ, NE, ND = 4096, 1024, 64, 6
WIN = NT + NE * ND
PW = NT + NE * (ND - 1)
TAIL_HI = NT + 3 * NE
ROUND4 = 3.0 * 2 ** 24
K1, V1 = 2560, 2048
VDEP = ["xk0", "xk0"]
KDEP = ""
VLAST = ""
VFIRST = ["", ""]
LATEB = False
ZN = 2
ZS = 704
XLAG = 0
LB = 768

SCRATCH = {
    "kwin": ("sbuf", [128, WIN], "bfloat16"), "vwin": ("sbuf", [128, WIN], "bfloat16"),
    "pwin": ("sbuf", [128, PW], "bfloat16"),
    "parc": ("sbuf", [128, 256], "int32"), "hi": ("sbuf", [128, 256], "bfloat16"), "lo": ("sbuf", [128, 256], "bfloat16"),
    "upc": ("sbuf", [128, 64], "int32"), "exs": ("sbuf", [128, 4], "int32"), "exl": ("sbuf", [128, 4], "int32"),
    "off": ("sbuf", [128, 8, 72], "uint16"), "xla": ("sbuf", [128, 24], "uint16"), "xlb": ("sbuf", [128, 24], "uint16"),
    "res": ("sbuf", [128, 6, 1088], "bfloat16"), "wf": ("sbuf", [128, 144], "float32"),
    "sel": ("sbuf", [128, 144], "bfloat16"), "cst": ("sbuf", [128, 256], "bfloat16"), "ehi": ("sbuf", [128, 20], "bfloat16"),
    "qs": ("sbuf", [128, NQ], "bfloat16"), "bs": ("sbuf", [128, 8], "float32"), "bb": ("sbuf", [128, 8], "bfloat16"),
    "nb": ("sbuf", [128, 8], "float32"),
    "tk": ("sbuf", [128, 6, NQ], "bfloat16"), "rl": ("sbuf", [128, 6, NQ], "bfloat16"),
    "fx": ("sbuf", [128, 6, NQ], "bfloat16"), "zz": ("sbuf", [128, NQ], "bfloat16"),
    "pr": ("sbuf", [128, 6, NQ], "float16"), "yo": ("sbuf", [128, NQ], "float32"),
    "xk": ("sbuf", [128, NE * ND], "bfloat16"), "xv": ("sbuf", [128, NE * ND], "bfloat16"),
    "accA": ("psum", [128, 512], "float32"), "accB1": ("psum", [128, 512], "float32"), "accB2": ("psum", [128, 512], "float32"),
    "chA": ("psum", [128, 512], "float32"), "chB": ("psum", [128, 512], "float32"),
    "a0": ("psum", [128, 512], "float32"), "a1": ("psum", [128, 512], "float32"), "a2": ("psum", [128, 512], "float32"),
}

TYPES = "VVVVSSVSSSSS"
MODE = "HHHAA"
CUT = 16
GK = [1, 1, 2, 2, 1, 2]
GR = [1, 1, 2, 2, 2, 2]
GV = [1, 2, 1, 2, 2, 2]
QE = False
QN = ["VS"] * 6
GQ = [[1, 1]] * 6
XE = "SSSSSSSSSSSSS"
KMSG = [[0], [1], [2], [3, 4, 5]]
VMSG = [[0, 1, 2], [3, 4, 5]]
FE = "SSV"
K1, GK, GR, GV, TYPES, CUT, KMSG, VMSG = 2048, [1, 1, 2, 2, 1, 2], [1, 1, 2, 2, 2, 2], [1, 1, 2, 2, 2, 2], "VVVVSSSSSSVS", 18, [[0], [1], [2], [3], [4, 5]], [[0, 1, 2], [3], [4, 5]]
ORDER = "msc Id nId C1Av C1As cpX P1A C1Bv C1Bs bb xk0 P1B mk0 dv1 dv2 cp1A C2Av C2As P2A cp1B C2Bv C2Bs xk1 mk1 P2B cp2A C3Av C3As P3A cp2B C3Bv C3Bs xk2 P3B cp3A mk2 xl02 C4As cp3B K1F C4Bs P4A xv0 P4B xv3 mv0 cp4A xk3 R1F C5As cp4B mk3 mv3 K2F C5Bs K3B P5B R2F K3A P5A cp5B xl45 V1F xk4 a3A xv4 mk4 K4B mv4 a3B V2F R3A a4B K4A R3B V3A s1A s1B1 a4A R4B V3B K5F cp5A V4B K6A R4A s1B2 s2A s2B1 s2B2 s3A s3B1 s3B2 s4B1 s4B2 a5A R6A K6B V4A a5B V6A R5A a6B R5B V5A R6B V5B s4A s6A s5A fA V6B1 V6B2 yA s5B1 s5B2 s6B1 fB1 fB2 yB1 yB2".split()
KDEP, K1, ZN, ZS, TYPES, GV = "l_ex", 2560, 1, 896, "VVVVVSSSSSVS", [1, 1, 2, 1, 2, 2]
ORDER = "msc Id nId C1As C1Av P1A cpX C1Bv C1Bs cp1A xk0 C2Av P1B C2As mk0 dv1 dv2 P2A cp1B C2Bv C2Bs cp2A xk1 P2B C3Av C3As mk1 P3A cp2B C3Bv C3Bs xl02 xk2 cp3A P3B bb C4As mk2 cp3B K1F xk3 P4A C4Bs mk3 xv0 P4B cp4A K3B R1F mv0 cp4B K3A C5Bs a3B K2F K4B P5B R3B a4B cp5B xl45 R2F xk4 xv3 mk4 R3A C5As V3A xv4 P5A V1F K4A mv3 mv4 R4B s3A a4A V2F K5F cp5A V3B R4A s1A s1B1 s1B2 a5A K6B a5B K6A R5A s2A a6B R6A V6A R5B R6B V4F V5A V5B s2B1 s2B2 s3B1 s3B2 s6A s4A s4B1 s4B2 s5A fA V6B1 yA V6B2 s5B1 s5B2 s6B1 fB1 fB2 yB1 yB2".split()
GK, GV, TYPES, MODE = [1, 1, 2, 2, 2, 2], [1, 2, 2, 1, 2, 2], "SVSSSSSVSSSZ", "HHHbb"
ORDER = "msc Id nId C1As C1Av P1A cpX C1Bv C1Bs bb xk0 P1B cp1A mk0 dv1 C2Av C2As dv2 P2A cp1B C2Bv C2Bs xk1 P2B mk1 cp2A C3Av C3As P3A cp2B C3Bv C3Bs xl02 xk2 P3B xv0 mk2 cp3A C4As cp3B P4A C4Bv xk3 xv3 mk3 K1A mv0 mv3 K1B P4B K2F cp4A a1A cp4B R1B K3A C5Bv a2B R1A P5B K4B K4A R2B a2A cp5B xl45 R4B xk4 V4B a4A mk4 R2A C5As a3A V1A K3B P5A V2B xv4 R4A mv4 a3B cp5A V2A R3A K5A V4A K6A s4B1 s4B2 s1A s2B1 a5A V3A K5B a6A R5A V1B R3B V5A R6A s2B2 s2A s4A a5B K6B V6A R5B s3A a6B V3B G6B R6B V5B s1B1 s1B2 s5A s6A fA V6B1 V6B2 yA s3B1 s3B2 s5B1 s5B2 fB2 s6B1 fB1 yB2 yB1".split()
LATEB, XLAG, K1, GK, GR, GV, TYPES, MODE = True, 1, 2048, [1, 1, 2, 1, 1, 2], [1, 2, 2, 2, 2, 2], [1, 1, 2, 1, 2, 2], "VVSSVSSSVSSS", "HHHHA"
ORDER = "msc Id nId C1Bs C1As C1Bv P1B C1Av cp1B cpX C2Bv P1A xk0 C2Bs P2B mk0 dv1 dv2 bb cp1A C2Av C2As P2A cp2B C3Bv C3Bs P3B cp2A C3Av cp3B C4Bv xk1 C3As P3A C4Bs mk1 P4B xl02 cp3A xk2 xv0 C4As C4Av cp4B P4A K1F C5Bs P5B cp5B xk3 K2F C6B mk2 K3B mv0 R1F P6B a2A a2B K3A cp4A R3A cp6B xl45 V3A V1F mk3 a3B C5As P5A xk4 xv3 R2B R2A mk4 mv3 K4F cp5A V2F K5A xv4 R3B R5A V3B s3A s1A s1B1 s1B2 a4A a4B mv4 R4A R4B K6A V4F K5B s2A s2B1 s2B2 s3B1 s3B2 a6A a5B R6A V5A V6A K6B R5B V5B s4A s4B1 s4B2 s5A a6B R6B s6A fA V6B1 yA V6B2 s5B1 s5B2 s6B1 fB1 fB2 yB1 yB2".split()
KDEP, VLAST, VDEP, GV, TYPES = "", "P1B", ["C2Bs", "C2Bs"], [1, 1, 1, 1, 2, 2], "VSVSVSSSVSSS"
ORDER = "msc Id nId C1Bs C1Bv C1As C1Av P1B cpX xk0 P1A mk0 cp1B C2Bv C2Bs dv1 dv2 cp1A P2B C2Av C2As P2A cp2B C3Bv C3Bs bb xk1 cp2A C3Av P3B C3As mk1 P3A cp3B C4Bv xk2 C4Bs mk2 xl02 K1A K1B P4B cp3A xv0 C4Av a1B C4As mv0 cp4B K2A C5Bs P4A K3A K2B P5B R2A R1B cp4A cp5B R1A C6B V1A xk3 P6B C5As mk3 R3A a2B K3B cp6B xl45 V3A P5A xk4 xv3 mk4 R2B V1B a3B xv4 K4F V2A mv3 mv4 cp5A V2B R3B s1A s3A s1B1 s1B2 s2A a4B K5A K6A a4A R5A R4B V3B s2B1 s2B2 a6A R4A V5A K5B V4F R6A s3B1 s3B2 s5A a5B K6B V6A R5B a6B V5B R6B V6B1 s4A s4B1 s4B2 s6A fA V6B2 yA s5B1 s5B2 fB2 s6B1 fB1 yB2 yB1".split()
HOOK = None

SEMAPHORES = ["s%d" % i for i in range(149)] + ["sent"]


def rank_program(g, core, T, topo):
    rank = T.rank_of(core)
    if rank is None:
        return
    N = len(T.cores)
    takes = rank > 0
    gives = rank < N - 1
    A, F = AluOpType, ActivationFunctionType
    Q = {"V": g.vector, "S": g.scalar, "P": g.tensor, "G": g, "Y": g.sync}
    ops = {}

    def add(name, q, fn, deps, inc=1):
        ops[name] = [q, fn, list(deps), inc]

    def dma(name, q, out, in_, deps):
        add(name, q, lambda: Q[q].dma_start(out, in_), deps, 16)

    sent = [0]
    landed = ["a_ex"] + ["a_k%d" % m[0] for m in KMSG] + ["a_v%d" % m[0] for m in VMSG]
    for s in range(1, ND + 1):
        for h in ("F" if TYPES[2 * s - 2:2 * s] == "XX" and GR[s - 1] == 1 else "AB"):
            if TYPES[2 * s - 2 + (h == "B")] == "X":
                landed += ["a_e%d%s" % (s, h), "a_h%d%s" % (s, h)]
    landed += [d for d in [KDEP] + VDEP if d.startswith("l_")]
    sem = {n: T.sem["s%d" % i] for i, n in enumerate(landed)}
    kdep = [KDEP] if takes and KDEP else []
    vdep = [([d] if gives else [VLAST]) if takes and d and (gives or VLAST) else [] for d in VDEP]
    if not takes:
        vdep = [[d] if d else [] for d in VFIRST]
    held = kdep + vdep[0] + vdep[1]

    def send(name, dst, out, in_, deps):
        rid, pid = topo.addr(dst)[0:2]
        if "l_" + name in held:
            arrive["l_" + name], left = len(topo.engines(core, dst)), sem["l_" + name]
        else:
            sent[0] += len(topo.engines(core, dst))
            left = T.sem.sent
        add("m" + name, "G", lambda: g.remote_dma(out, in_, sem["a_" + name], left, pid, rid, topo.mask(core, dst)), deps, 0)

    twin = [c for c in T.cores if c != core and topo.chip(c) == topo.chip(core)][0]

    def fold(name, out, srcs, op, deps):
        rid, pid = topo.addr(twin)[0:2]
        sent[0] += len(topo.engines(core, twin))
        arrive["a_" + name] = len(topo.engines(twin, core))
        add("m" + name, "G", lambda: g.remote_dma_fused(
            [RemoteDMATransfer(dst_ids=[DstId(rid=rid, pnc=pid)], dma_engine_mask=topo.mask(core, twin), remote_sem=sem["a_" + name],
                               srcs=srcs, dsts=[out], alu_op=op)], local_sem=T.sem.sent), deps, 0)

    arrive = {}
    if gives:
        arrive["a_ex"] = len(topo.engines(T.cores[rank + 1], core))
    if takes:
        for a in ["a_k%d" % m[0] for m in KMSG] + ["a_v%d" % m[0] for m in VMSG]:
            arrive[a] = len(topo.engines(T.cores[rank - 1], core))

    def gather(e, out, win, offs):
        if e == "V":
            return lambda: g.vector.tensor_copy(out, win.indirect(offs))
        return lambda: g.scalar.activation(out, win.indirect(offs), F.Copy)

    Id, nId = T.cst[:, 0:128], T.cst[:, 128:256]

    if takes:
        dma("dex", "S", T.exs[:], T.ex[:], [])
    dma("dpar", "Y", T.parc[:], T.par[:], [])
    dma("dup", "S", T.upc[:], T.up[:], [])
    if QE:
        dma("db", "S", T.bs[:, 0:ND], T.b[:], [])
        dma("dq", "Y", T.qs[:], T.q[:], [])
    dma("dk1", "Y", T.kwin[:, 0:K1], T.k[:, 0:K1], [])
    add("ms0", "V", lambda: g.vector.memset(T.pwin[:, 0:ZS], 0.0), [])
    win = ["dhi", "dlo"]
    if takes:
        add("mse", "V", lambda: g.vector.memset(T.ehi[:], float(TAIL_HI)), [])
        add("io", "G", lambda: g.iota(T.pwin[:, NT:PW], [[1, PW - NT]], NT + NE - TAIL_HI, 0, allow_small_or_imprecise_dtypes=True), [])
        win.append("dehi")
    add("ms", "V", lambda: g.vector.memset(T.pwin[:, ZS:NT - ZN * ZS], 0.0), [])
    clear = ["ms", "mss"]
    if ZN == 2:
        add("mss0", "S", lambda: g.scalar.activation(T.pwin[:, NT - 2 * ZS:NT - ZS], T.pwin[:, 0:ZS], F.Copy), ["ms0"])
        clear.append("mss0")
    else:
        add("mss", "S", lambda: g.scalar.activation(T.pwin[:, NT - ZS:NT], T.pwin[:, 0:ZS], F.Copy), ["ms0"])
    add("iw", "G", lambda: g.iota(T.wf[:], [[-32, 9], [-2000, 16]], 31, 2, allow_small_or_imprecise_dtypes=True), [])
    if takes:
        dma("dehi", "Y" if LATEB else "S", T.pwin[0:128:16, NT:PW], T.ehi[:], ["io", "mse"])
        send("ex", T.cores[rank - 1], T.exl[:], T.exs[:], ["dex"])
    if ZN == 2:
        add("mss", "S", lambda: g.scalar.activation(T.pwin[:, NT - ZS:NT], T.pwin[:, 0:ZS], F.Copy), ["ms0"])
    if not QE and not LATEB:
        dma("db", "S", T.bs[:, 0:ND], T.b[:], [])
    add("hi", "V", lambda: g.vector.tensor_copy(T.hi[:], T.parc[:]), ["dpar"])
    dma("dhi", "Y", T.pwin[0:128:16, 0:NT], T.hi[:], ["hi"] + clear)
    add("lo", "V", lambda: g.vector.tensor_tensor(T.lo[:], T.parc[:], T.hi[:], A.subtract), ["hi"])
    dma("dlo", "Y", T.pwin[1:128:16, 0:NT], T.lo[:], ["lo"] + clear)
    if K1 < NT:
        dma("dk2", "Y", T.kwin[:, K1:NT], T.k[:, K1:NT], kdep)
    if not QE:
        dma("dq", "Y", T.qs[:], T.q[:], kdep)
        if LATEB:
            dma("db", "Y", T.bs[:, 0:ND], T.b[:], [])
    add("W", "V", lambda: g.vector.tensor_scalar(T.sel[:], T.wf[:], ROUND4, ROUND4, A.add, A.is_equal), ["iw"])
    add("cpU", "V", lambda: g.vector.tensor_copy(T.off[:, 1, 0:64], T.upc[:]), ["dup"])
    pre = list(ops)
    add("msc", "V", lambda: g.vector.memset(T.cst[:], 0.0), [])
    if "X" in TYPES:
        add("msz", "V", lambda: g.vector.memset(T.zz[:], 0.0), [])
    add("bb", "V", lambda: g.vector.tensor_copy(T.bb[:, 0:ND], T.bs[:, 0:ND]), ["db"])
    if "M" in TYPES:
        add("nb", "S", lambda: g.scalar.activation(T.nb[:, 0:ND], T.bs[:, 0:ND], F.Copy, scale=-1.0), ["db"])
    add("Id", "G", lambda: g.affine_select(Id, Id, [[-1, 128]], A.not_equal, 1.0, 0, 1), ["msc"])
    add("nId", "G", lambda: g.affine_select(nId, nId, [[-1, 128]], A.not_equal, -1.0, 0, 1), ["msc"])
    for j, (a, b) in enumerate(((0, V1), (V1, NT))):
        dma("dv%d" % (j + 1), "Y", T.vwin[:, a:b], T.v[:, a:b], vdep[j])
    ld = {"k": ["dk1", "dk2"][0:1 + (K1 < NT)], "v": ["dv1", "dv2"]}

    def ready(s, h):
        if s == 1:
            return ["cpU"]
        if s == 7:
            return ["cp6B"]
        if MODE[s - 2] in "FSV":
            return ["cp%dF" % (s - 1)]
        return ["cp%d%s" % (s - 1, x) for x in ("AB" if h == "F" else h)]

    def xready(t):
        return ["cpX"] if t == 0 else ready(t + 1 + XLAG, "B")

    pwin = T.pwin[:, 0:(PW if takes else NT)]

    def relay(name, s, c0, c1, r0, ps, deps):
        n = c1 - c0

        def emit():
            for i in range(16):
                ins = g.tensor.matmul(ps[:, 0:n], T.sel[:, 16 - i:144 - i], T.res[:, s - 1, r0 + i:r0 + 16 * n:16], i == 0, i == 15)
            return ins
        add("P" + name, "P", emit, deps + ["W"])
        add("cp" + name, "V", lambda: g.vector.tensor_copy(T.off[:, s + 1, c0:c1], ps[:, 0:n]), ["P" + name])

    if gives:
        add("cpX", "V", lambda: g.vector.tensor_copy(T.off[:, 1 + XLAG, 64:68], T.exl[:]), ["a_ex"])
    for s in range(1, ND):
        m = MODE[s - 1]
        end = 68 if (s > XLAG and gives) else 64
        for h in ("F" if m in "FSV" else "AB"):
            c0, c1 = {"F": (0, end), "A": (0, 32), "B": (32, end)}[h]
            d = ready(s, h) + win + (["cpX"] if s == 1 + XLAG and h != "A" and gives else [])
            es = {"H": "vs", "F": "vs", "S": "s", "A": "s", "V": "v", "W": "v", "B": "v" if h == "A" else "s", "b": "s" if h == "A" else "v"}[m]
            cuts = [c0, c1] if len(es) == 1 else [c0, c0 + CUT * (2 if h == "F" else 1), c1]
            for j, e in enumerate(es):
                a, b = cuts[j], cuts[j + 1]
                add("C%d%s%s" % (s, h, e), e.upper(), gather(e.upper(), T.res[:, s - 1, 16 * a:16 * b], pwin, T.off[:, s, a:b]), d)
            relay("%d%s" % (s, h), s, c0, c1, 16 * c0, T.chB if h == "B" else T.chA, ["C%d%s%s" % (s, h, e) for e in es])
    if gives and XLAG:
        add("C6B", XE[12], gather(XE[12], T.res[:, 5, 0:64], pwin, T.off[:, 6, 64:68]), ready(6, "B"))
        relay("6B", 6, 64, 68, 0, T.chB, ["C6B"])

    arr = {"k": {}, "v": {}}
    lists = {}
    for nm, msgs, wn, st in (("k", KMSG, T.kwin, T.xk), ("v", VMSG, T.vwin, T.xv)):
        for m in msgs:
            a, b = m[0], m[-1] + 1
            for t in m:
                arr[nm][t] = "a_%s%d" % (nm, a)
            if not gives:
                continue
            if len(m) > 1:
                key = "xl%d%d" % (a, b - 1)
                if key not in lists:
                    xl = (T.xla if nm == "k" else T.xlb)[:, 4 * a:4 * b]
                    lists[key] = xl
                    add(key, "V", (lambda o, i: lambda: g.vector.tensor_copy(o, i))(xl, T.off[:, a + 1 + XLAG:b + 1 + XLAG, 64:68]),
                        sum([xready(t) for t in m], []))
                d, offs = [key], lists[key]
            else:
                d, offs = xready(a), T.off[:, a + 1 + XLAG, 64:68]
            e = XE[a + (6 if nm == "v" else 0)]
            add("x%s%d" % (nm, a), e, gather(e, st[:, NE * a:NE * b], wn[:, 0:NT], offs), d + ld[nm])
            send("%s%d" % (nm, a), T.cores[rank + 1], wn[:, NT + NE * a:NT + NE * b], st[:, NE * a:NE * b], ["x%s%d" % (nm, a)])

    banks = [T.a0[:, 0:512], T.a1[:, 0:512], T.a2[:, 0:512]]
    bank = {}
    cols = {"F": (0, 1024), "A": (0, 512), "B": (512, 1024), "B1": (512, LB), "B2": (LB, 1024),
            "a": (0, 256), "b": (256, 512), "c": (512, 768), "d": (768, 1024)}
    acc = {"A": T.accA[:, 0:512], "B1": T.accB1[:, 0:LB - 512], "B2": T.accB2[:, 0:1024 - LB]}
    fe = dict(zip(("A", "B1", "B2"), FE))
    sums = {}
    ends = {}

    def level(s):
        ty = {"A": TYPES[2 * s - 2], "B": TYPES[2 * s - 1]}
        same = ty["A"] == ty["B"]
        wcols = NT + NE * s if takes else NT
        kw, vw = T.kwin[:, 0:wcols], T.vwin[:, 0:wcols]
        came = {x: (sorted(set(arr[x][i] for i in range(s))) if takes else []) for x in "kv"}
        bcol, bbcol = T.bs[:, s - 1:s], T.bb[:, s - 1:s]
        vd = ld["v"] + came["v"]
        made = {"K": {}, "R": {}, "Q": {}, "N": {}}

        def half(part):
            return "A" if cols[part][0] < 512 else "B"

        def over(kind, part):
            return [n for x, n in made[kind].items() if cols[x][0] < cols[part][1] and cols[part][0] < cols[x][1]]

        def keys(part):
            n, t = "K%d%s" % (s, part), ty[half(part)]
            c0, c1 = cols[part]
            offs, tk, qq = T.off[:, s, c0 // 16:c1 // 16], T.tk[:, s - 1, c0:c1], T.qs[:, c0:c1]
            kd = ready(s, "F" if part == "F" else half(part)) + ld["k"] + came["k"]
            if t == "M":
                add(n, "V", lambda: g.vector.tensor_tensor(tk, kw.indirect(offs), T.rl[:, s - 1, c0:c1], A.min), kd + over("Q", part))
            elif t in "VW":
                add(n, "V", lambda: g.vector.tensor_tensor(tk, kw.indirect(offs), qq, A.subtract), kd + ["dq"])
            elif t in "DU":
                add(n, "S", lambda: g.scalar.activation(tk, kw.indirect(offs), F.Copy, scale=-1.0), kd)
            elif t == "X":
                add(n, "S", lambda: g.scalar.activation(tk, kw.indirect(offs), F.Identity, bias=bcol, scale=-1.0), kd + ["db"])
            else:
                add(n, "S", gather("S", tk, kw, offs), kd)
            made["K"][part] = n

        def relu(part):
            n, t = "%d%s" % (s, part), ty[half(part)]
            c0, c1 = cols[part]
            tk, rl, qq = T.tk[:, s - 1, c0:c1], T.rl[:, s - 1, c0:c1], T.qs[:, c0:c1]
            made["R"][part] = "R" + n
            if t == "V":
                add("R" + n, "V", lambda: g.vector.tensor_scalar(rl, tk, bbcol, 0.0, A.subtract, A.min), over("K", part) + ["bb"])
            elif t == "W":
                add("R" + n, "S", lambda: g.scalar.activation(rl, tk, F.Relu, bias=bcol, scale=-1.0), over("K", part) + ["db"])
            elif t in "DU":
                add("d" + n, "G", lambda: g.dma_start(tk, qq, accum_op=A.add), over("K", part) + ["dq"], 16)
                if t == "D":
                    add("R" + n, "V", lambda: g.vector.tensor_scalar(rl, tk, bbcol, 0.0, A.add, A.max), ["d" + n, "bb"])
                else:
                    add("R" + n, "S", lambda: g.scalar.activation(rl, tk, F.Relu, bias=bcol), ["d" + n, "db"])
            elif t == "M":
                add("d" + n, "G", lambda: g.dma_start(tk, T.fx[:, s - 1, c0:c1], accum_op=A.add), over("K", part) + over("N", part), 16)
                made["R"][part] = "d" + n
            elif t == "X":
                fx = T.fx[:, s - 1, c0:c1]
                fold("e" + n, fx, [tk, qq], 1, over("K", part) + ["dq"])
                fold("h" + n, rl, [fx, T.zz[:, c0:c1]], 2, ["a_e" + n, "msz"])
                made["R"][part] = "a_h" + n
            else:
                def emit():
                    g.tensor.matmul(bank[n], Id, qq, True, False)
                    return g.tensor.matmul(bank[n], nId, tk, False, True)
                add("a" + n, "P", emit, over("K", part) + ["dq", "Id", "nId"])
                if t == "T":
                    add("R" + n, "V", lambda: g.vector.tensor_scalar(rl, bank[n], bcol, 0.0, A.add, A.max), ["a" + n, "db"])
                else:
                    add("R" + n, "S", lambda: g.scalar.activation(bank[n] if t == "Z" else rl, bank[n], F.Relu, bias=bcol), ["a" + n, "db"])
                if t == "Z":
                    add("G" + n, "S", gather("S", rl, vw, T.off[:, s, c0 // 16:c1 // 16]), ready(s, part) + vd)

        def ahead(kind, part, e):
            c0, c1 = cols[part]
            n, qq = "%s%d%s" % (kind, s, part), T.qs[:, c0:c1]
            out, sign = (T.rl[:, s - 1, c0:c1], 1.0) if kind == "Q" else (T.fx[:, s - 1, c0:c1], -1.0)
            if e == "V":
                add(n, "V", lambda: g.vector.tensor_scalar(out, qq, bbcol, sign, A.add, A.mult), ["dq", "bb"])
            elif kind == "Q":
                add(n, "S", lambda: g.scalar.activation(out, qq, F.Identity, bias=bcol), ["dq", "db"])
            else:
                add(n, "S", lambda: g.scalar.activation(out, qq, F.Identity, bias=T.nb[:, s - 1:s], scale=-1.0), ["dq", "nb"])
            made[kind][part] = n

        for kind, e, n in zip("QN", QN[s - 1], GQ[s - 1]):
            for part in {1: "F" if same else "AB", 2: "AB", 4: "abcd"}[n]:
                if ty[half(part)] == "M":
                    ahead(kind, part, e)
        for part in {1: "F" if same else "AB", 2: "AB", 4: "abcd"}[GK[s - 1]]:
            keys(part)
        for part in ("F" if same and GR[s - 1] == 1 and ty["A"] in "VWDUXM" else "AB"):
            relu(part)
        fv = s < ND and GV[s - 1] == 1 and len({(t in "VM", t == "M") for t in ty.values()}) == 1 and "Z" not in ty.values()

        def product(part):
            c0, c1 = cols[part]
            name, h = "V%d%s" % (s, part), half(part)
            pr, rl, n = T.pr[:, s - 1, c0:c1], (T.tk if ty[h] == "M" else T.rl)[:, s - 1, c0:c1], "%d%s" % (s, h)
            if ty[h] == "Z":
                b0 = c0 - cols[h][0]
                add(name, "V", lambda: g.vector.tensor_tensor(pr, rl, bank[n][:, b0:b0 + c1 - c0], A.mult), ["G" + n, "R" + n])
            else:
                add(name, "V", lambda: g.vector.tensor_tensor(pr, vw.indirect(T.off[:, s, c0 // 16:c1 // 16]), rl, A.mult),
                    vd + over("R", part))
            neg = ty[h] in "VM"
            for b in {"F": ["A", "B1", "B2"], "B": ["B1", "B2"]}.get(part, [part]):
                if s == ND and fe[b] == "V":
                    sums["last" + b] = (name, neg)
                else:
                    add_sum("s%d%s" % (s, b), b, neg, name)

        def add_sum(n, b, neg, dep):
            c0, c1 = cols[b]
            add(n, "P", lambda: g.tensor.matmul(acc[b], nId if neg else Id, T.pr[:, s - 1, c0:c1], ends[n][0], ends[n][1]), [dep, "Id", "nId"])
            sums.setdefault(b, []).append(n)

        for part in ("F" if fv else ("A", "B") if s < ND else ("A", "B1", "B2")):
            product(part)

    for s in range(1, ND + 1):
        level(s)

    def empty(b, q):
        c0, c1 = cols[b]
        if fe[b] == "V":
            name, neg = sums["last" + b]
            add("f" + b, "V", lambda: g.vector.tensor_tensor(T.yo[:, c0:c1], acc[b], T.pr[:, ND - 1, c0:c1],
                                                             A.subtract if neg else A.add), sums[b] + [name])
        else:
            add("f" + b, "S", lambda: g.scalar.activation(T.yo[:, c0:c1], acc[b], F.Copy), sums[b])
        dma("y" + b, q, T.y[:, c0:c1], T.yo[:, c0:c1], ["f" + b])

    empty("A", "Y")
    empty("B1", "S" if fe["B1"] == "S" else "Y")
    empty("B2", "Y")

    if HOOK is not None:
        for n in ops:
            if n[0] == "a":
                bank[n[1:]] = banks[0]
            if n[0] == "s":
                ends[n] = (True, True)
        HOOK[rank] = (ops, pre, arrive)
        return

    order = pre + [n for n in ORDER if n in ops]
    forms = [n for n in order if n[0] == "a"]
    for j, n in enumerate(forms):
        bank[n[1:]] = banks[j % 3]
        if j >= 3:
            w = forms[j - 3][1:]
            ops[n][2].extend([x for x in ops if x.startswith("V" + w)] if "G" + w in ops else ["R" + w])
    for b in acc:
        seq = [n for n in order if n in sums[b]]
        for n in seq:
            ends[n] = (n == seq[0], n == seq[-1])
        ops["f" + b][2] = [d for d in ops["f" + b][2] if d not in seq[:-1]]
    for q in "YS":
        add("end" + q, q, None, [n for n in order if n[0] == "y" and ops[n][0] == q])
        order.append("end" + q)
    assert sorted(order) == sorted(ops)

    known = {q: set() for q in Q}
    behind = {a: set() for a in arrive}
    waits = {}
    pos = {n: i for i, n in enumerate(order)}
    for n in order:
        q, fn, deps, inc = ops[n]
        waits[n] = []
        for d in sorted(set(deps), key=lambda x: -pos.get(x, -1)):
            if d not in known[q]:
                waits[n].append(d)
                known[q] |= behind[d] | {d}
        behind[n] = set(known[q])
    waited = [n for n in order if any(n in w for w in waits.values())]
    for i, n in enumerate(waited):
        sem[n] = T.sem["s%d" % (len(landed) + i)]
    for n in order:
        q, fn, deps, inc = ops[n]
        for d in waits[n]:
            Q[q].wait_ge(sem[d], arrive[d] if d in arrive else ops[d][3])
        if fn is not None:
            ins = fn()
            if n in waited:
                ins.then_inc(sem[n], inc)
    if sent[0]:
        g.wait_ge(T.sem.sent, sent[0])
